import numpy as np
import ml_dtypes


def mxq(x, axis, fmt="e4m3"):
    dtype, down = {"e4m3": (ml_dtypes.float8_e4m3fn, 7), "e5m2": (ml_dtypes.float8_e5m2, 14)}[fmt]
    v = np.moveaxis(np.asarray(x, np.float32).astype(ml_dtypes.bfloat16).astype(np.float64), axis, -1)
    blocks = v.reshape(v.shape[:-1] + (-1, 32))
    amax = np.abs(blocks).max(-1, keepdims=True)
    byte = np.maximum(np.where(amax > 0, np.frexp(amax)[1] - 1 + 127, 0) - down, 1)
    scale = np.exp2(byte - 127.0)
    codes = (blocks / scale).astype(np.float32).astype(dtype).astype(np.float64)
    return np.moveaxis((codes * scale).reshape(v.shape), -1, axis)


WIDE = False


def mx_kscale(k):
    if not WIDE:
        return np.ones(k)
    levels = np.array([10, -10, 5, -5, 0])
    if k % 512:
        return np.exp2(np.random.permutation(np.resize(levels, k // 32))).repeat(32)
    a = np.empty((k // 512, 16))
    for p in range(k // 512):
        a[p, :8] = np.random.permutation(np.resize(levels, 8))
        for g in range(8):
            far = levels[np.abs(levels - a[p, g]) >= 10]
            a[p, g + 8] = far[np.random.randint(len(far))]
    return np.exp2(a.ravel()).repeat(32)


def f64(x):
    return np.asarray(x).astype(np.float64)


def striped(idx):
    return np.tile(idx.reshape(-1, 16).T, (8, 1)).astype(np.uint16)


def unstriped(offs):
    return offs[:16].T.reshape(-1).astype(np.int64)


E2M1 = np.array([0.0, 0.5, 1.0, 1.5, 2.0, 3.0, 4.0, 6.0, -0.0, -0.5, -1.0, -1.5, -2.0, -3.0, -4.0, -6.0])


def pack_fp4(w):
    k, n = w.shape
    w = f64(np.asarray(w, np.float32).astype(ml_dtypes.bfloat16)).reshape(k // 32, 32, n)
    amax = np.abs(w).max(1)
    mant, ex = np.frexp(amax / 6.0)
    byte = np.clip(np.where(amax > 0, np.where(mant > 0.5, ex, ex - 1) + 127, 1), 1, 254)
    scaled = (w * np.exp2(127.0 - byte)[:, None, :]).reshape(k, n).astype(np.float32)
    c = np.ascontiguousarray(scaled.reshape(k // 512, 128, 4, n).transpose(0, 1, 3, 2)).astype(ml_dtypes.float4_e2m1fn).view(np.uint8) & 0xF
    words = (c[..., 0::2] | (c[..., 1::2] << 4)).reshape(k // 512, 128, 2 * n)
    return np.ascontiguousarray(words), np.ascontiguousarray(byte.astype(np.uint8).reshape(k // 512, 16, n))


def unpack_fp4(words, scales):
    g, _, n = scales.shape
    words = np.ascontiguousarray(words).reshape(g, 128, n, 2)
    nib = np.empty((g, 128, n, 4), np.uint8)
    nib[..., 0::2] = words & 0xF
    nib[..., 1::2] = words >> 4
    vals = E2M1[nib] * np.repeat(np.exp2(scales.astype(np.float64) - 127.0), 8, axis=1)[..., None]
    return vals.transpose(0, 1, 3, 2).reshape(g * 512, n)


def silu(v):
    return v / (1.0 + np.exp(-np.maximum(v, -700.0)))


K, T, S, H, N = 512, 2048, 1024, 512, 128
P = 2 ** 7


def setup_inputs():
    n = np.random.standard_normal
    s = mx_kscale(K)[:, None]
    u = mx_kscale(H)
    packed_w2 = pack_fp4(n((H, N)) / np.sqrt(H) / u[:, None])
    return {
        "xT": (n((K, T)) * s).astype(np.float32),
        "gate": np.tile(np.random.uniform(0.2, 1.0, S), (P, 1)).astype(np.float32),
        "res": n((N, T)).astype(np.float32),
        "w1": (n((K, H)) / np.sqrt(K) / s).astype(np.float32),
        "w3": (n((K, H)) / np.sqrt(K) / s * u).astype(np.float32),
        "w2_words": packed_w2[0],
        "w2_scales": packed_w2[1],
        "offs": striped(np.random.permutation(T)[:S]),
    }


def reference(xT, gate, res, w1, w3, w2_words, w2_scales, offs):
    r = f64(res)[:, unstriped(offs)]
    xq = mxq(f64(xT)[:, unstriped(offs)], 0, "e4m3")
    h = (silu(mxq(f64(w1), 0, "e4m3").T @ xq)) * ((mxq(f64(w3), 0, "e4m3").T @ xq))
    y = unpack_fp4(w2_words, w2_scales).T @ mxq(h, 0, "e4m3")
    out = f64(res).copy()
    out[:, unstriped(offs)] = r + y * f64(gate)[:1]
    return out

@@ -1,0 +1,145 @@
+from contextlib import ExitStack
+
+import concourse.mybir as mybir
+
+K, T, S, H, N = 512, 2048, 1024, 512, 128
+FLOPS = 2 * S * (2 * K * H + H * N)
+
+F32 = mybir.dt.float32
+BF16 = mybir.dt.bfloat16
+I32 = mybir.dt.int32
+U32 = mybir.dt.uint32
+U16 = mybir.dt.uint16
+U8 = mybir.dt.uint8
+FP8X4 = mybir.dt.float8_e4m3fn_x4
+FP4X4 = mybir.dt.float4_e2m1fn_x4
+ALU = mybir.AluOpType
+ACT = mybir.ActivationFunctionType
+
+P = 128
+PACK = 4
+PIECE = 512
+HALF = S // 2
+CHUNK = 128
+
+
+def tile_picked_modres_glusilu_l_kernel(tc, xT, gate, res, w1, w3, w2_words, w2_scales, offs, out):
+    nc = tc.nc
+    with ExitStack() as ctx:
+        keep = ctx.enter_context(tc.tile_pool(name="keep", bufs=1))
+        psum_up = ctx.enter_context(tc.psum_pool(name="psum_up", bufs=3))
+        psum_down = ctx.enter_context(tc.psum_pool(name="psum_down", bufs=2))
+
+        offsets = keep.tile([P, S // 16], U16, name="offsets")
+        x_rows = xT.rearrange("(p j) n -> p j n", j=PACK)
+        pieces = T // PIECE
+        raw = {}
+        for u in range(2):
+            for q in range(pieces):
+                raw[u, q] = keep.tile([P, 2, PIECE], F32, name=f"x_raw{u}{q}")
+                nc.sync.dma_start(raw[u, q][:], x_rows[:, 2 * u : 2 * u + 2, q * PIECE : (q + 1) * PIECE])
+                if (u, q) == (0, 0):
+                    nc.sync.dma_start(offsets[:], offs)
+        w_raw = {}
+        for i, w in enumerate((w1, w3)):
+            w_rows = w.rearrange("(p j) c -> p j c", j=PACK)
+            for g in range(2):
+                w_raw[i, g] = keep.tile([P, PACK, H // 2], F32, name=f"w_raw{i}{g}")
+                nc.sync.dma_start(w_raw[i, g][:], w_rows[:, :, g * (H // 2) : (g + 1) * (H // 2)])
+        window = keep.tile([P, T], F32, name="window")
+        nc.sync.dma_start(window[:], res)
+        gate_sb = keep.tile([P, S], F32, name="gate_sb")
+        nc.sync.dma_start(gate_sb[:], gate)
+
+        w2_codes = keep.tile([P, 2 * N], U8, name="w2_codes", align_bytes=64)
+        w2_plane = keep.tile([P, N], U8, name="w2_plane", align_bytes=64)
+        nc.gpsimd.memset(w2_plane[:].bitcast(I32), 0)
+        nc.gpsimd.dma_start(w2_codes[:].bitcast(I32), w2_words[0].bitcast(I32))
+        for q in range(4):
+            nc.gpsimd.dma_start(w2_plane[32 * q : 32 * q + 4, :].bitcast(I32), w2_scales[0, 4 * q : 4 * q + 4, :].bitcast(I32))
+
+        picked = [keep.tile([P, HALF, 2], U32, name=f"picked{g}", align_bytes=64) for g in range(2)]
+        for u in range(2):
+            pairs = keep.tile([P, T], U32, name=f"pairs{u}")
+            for q in range(pieces):
+                dst = pairs[:, q * PIECE : (q + 1) * PIECE].bitcast(BF16).rearrange("p (n j) -> p n j", j=2)
+                src = raw[u, q][:].rearrange("p j n -> p n j")
+                if u == 0 or q == pieces - 1:
+                    nc.vector.tensor_copy(dst, src)
+                else:
+                    nc.scalar.copy(dst, src)
+            for g in range(2):
+                nc.vector.tensor_copy(picked[g][:, :, u], pairs[:].indirect(offsets[:, g * (HALF // 16) : (g + 1) * (HALF // 16)]))
+
+        x_codes = [keep.tile([P, HALF], U32, name=f"x_codes{g}", align_bytes=64) for g in range(2)]
+        x_plane = [keep.tile([P, HALF], U8, name=f"x_plane{g}", align_bytes=64) for g in range(2)]
+        for g in range(2):
+            nc.vector.quantize_mx(
+                out=x_codes[g][:].bitcast(FP8X4),
+                scales=x_plane[g][:],
+                in_=picked[g][:].rearrange("p n u -> p (n u)").bitcast(BF16),
+            )
+
+        w_codes, w_plane = [], []
+        for i in range(2):
+            grouped = keep.tile([P, PACK * H], BF16, name=f"w_grouped{i}", align_bytes=64)
+            for g in range(2):
+                dst = grouped[:].rearrange("p (t m j) -> p m t j", t=PACK, j=PACK)[:, g * 64 : (g + 1) * 64, :, :]
+                src = w_raw[i, g][:].rearrange("p j (m t) -> p m t j", t=PACK)
+                if (i, g) == (1, 1):
+                    nc.vector.tensor_copy(dst, src)
+                else:
+                    nc.scalar.copy(dst, src)
+            codes = keep.tile([P, H], U32, name=f"w_codes{i}", align_bytes=64)
+            plane = keep.tile([P, H], U8, name=f"w_plane{i}", align_bytes=64)
+            nc.vector.quantize_mx(out=codes[:].bitcast(FP8X4), scales=plane[:], in_=grouped[:])
+            w_codes.append(codes)
+            w_plane.append(plane)
+
+        def up(i, g, c):
+            acc = psum_up.tile([P, PACK, CHUNK], F32, name=f"up{i}")
+            cols = slice(c * CHUNK, (c + 1) * CHUNK)
+            for t in range(PACK):
+                nc.tensor.matmul_mx(
+                    out=acc[:, t, :],
+                    lhsT=w_codes[i][:, t * P : (t + 1) * P].bitcast(FP8X4),
+                    lhsT_scale=w_plane[i][:, t * P : (t + 1) * P],
+                    rhs=x_codes[g][:, cols].bitcast(FP8X4),
+                    rhs_scale=x_plane[g][:, cols],
+                    start=True,
+                    stop=True,
+                )
+            return acc[:].rearrange("p t n -> p n t")
+
+        gated = []
+        for g in range(2):
+            hidden = keep.tile([P, HALF, PACK], BF16, name=f"hidden{g}", align_bytes=64)
+            for c in range(HALF // CHUNK):
+                act = keep.tile([P, CHUNK, PACK], F32, name=f"act{g}{c}")
+                nc.scalar.activation(act[:], up(0, g, c), ACT.Silu)
+                nc.vector.tensor_tensor(hidden[:, c * CHUNK : (c + 1) * CHUNK, :], up(1, g, c), act[:], ALU.mult)
+            h_codes = keep.tile([P, HALF], U32, name=f"h_codes{g}", align_bytes=64)
+            h_plane = keep.tile([P, HALF], U8, name=f"h_plane{g}", align_bytes=64)
+            nc.vector.quantize_mx(out=h_codes[:].bitcast(FP8X4), scales=h_plane[:], in_=hidden[:].rearrange("p n t -> p (n t)"))
+            y = psum_down.tile([P, HALF], F32, name="y")
+            nc.tensor.matmul_mx(
+                out=y[:],
+                lhsT=w2_codes[:].bitcast(FP4X4),
+                lhsT_scale=w2_plane[:],
+                rhs=h_codes[:].bitcast(FP8X4),
+                rhs_scale=h_plane[:],
+                start=True,
+                stop=True,
+            )
+            gated.append(y)
+
+        old = keep.tile([P, S], F32, name="old")
+        nc.vector.tensor_copy(old[:], window[:].indirect(offsets[:]))
+        for g in range(2):
+            cols = slice(g * HALF, (g + 1) * HALF)
+            update = keep.tile([P, HALF], F32, name=f"update{g}")
+            nc.vector.tensor_tensor(update[:], gated[g][:], gate_sb[:, cols], ALU.mult)
+            nc.vector.tensor_tensor(
+                window[:].indirect(offsets[:, g * (HALF // 16) : (g + 1) * (HALF // 16)]), old[:, cols], update[:], ALU.add
+            )
+        nc.sync.dma_start(out, window[:])

@@ -1,6 +1,7 @@
 from contextlib import ExitStack
 
 import concourse.mybir as mybir
+from concourse.masks import make_identity
 
 K, T, S, H, N = 512, 2048, 1024, 512, 128
 FLOPS = 2 * S * (2 * K * H + H * N)
@@ -18,7 +19,11 @@ ACT = mybir.ActivationFunctionType
 
 P = 128
 PACK = 4
-PIECE = 512
+X_PIECES = (
+    ((0, 1024), (1024, 1536), (1536, 1792), (1792, 2048)),
+    ((0, 512), (512, 1024), (1024, 1536), (1536, 1792), (1792, 2048)),
+)
+W_PIECES = (((0, 256), (256, 512)), ((0, 256), (256, 384), (384, 512)))
 HALF = S // 2
 CHUNK = 128
 
@@ -28,73 +33,82 @@ def tile_picked_modres_glusilu_l_kernel(tc, xT, gate, res, w1, w3, w2_words, w2_
     with ExitStack() as ctx:
         keep = ctx.enter_context(tc.tile_pool(name="keep", bufs=1))
         psum_up = ctx.enter_context(tc.psum_pool(name="psum_up", bufs=3))
-        psum_down = ctx.enter_context(tc.psum_pool(name="psum_down", bufs=2))
+        psum_down = ctx.enter_context(tc.psum_pool(name="psum_down", bufs=1))
 
         offsets = keep.tile([P, S // 16], U16, name="offsets")
         x_rows = xT.rearrange("(p j) n -> p j n", j=PACK)
-        pieces = T // PIECE
+        w2_codes = keep.tile([P, 2 * N], U8, name="w2_codes", align_bytes=64)
+        w2_plane = keep.tile([P, N], U8, name="w2_plane", align_bytes=64)
+        gate_rows = keep.tile([P, P], F32, name="gate_rows")
+        identity = keep.tile([P, P], F32, name="identity")
+        warm = keep.tile([P, 2], F32, name="warm")
+        nc.gpsimd.memset(warm[:, 0:1], 0.0)
+        nc.scalar.activation(warm[:, 1:2], warm[:, 0:1], ACT.Silu)
+        nc.gpsimd.memset(w2_plane[:].bitcast(I32), 0)
+        nc.gpsimd.memset(gate_rows[:], 0.0)
+        make_identity(nc, identity[:])
         raw = {}
         for u in range(2):
-            for q in range(pieces):
-                raw[u, q] = keep.tile([P, 2, PIECE], F32, name=f"x_raw{u}{q}")
-                nc.sync.dma_start(raw[u, q][:], x_rows[:, 2 * u : 2 * u + 2, q * PIECE : (q + 1) * PIECE])
+            for q, (lo, hi) in enumerate(X_PIECES[u]):
+                raw[u, q] = keep.tile([P, 2, hi - lo], F32, name=f"x_raw{u}{q}")
+                nc.sync.dma_start(raw[u, q][:], x_rows[:, 2 * u : 2 * u + 2, lo:hi])
                 if (u, q) == (0, 0):
                     nc.sync.dma_start(offsets[:], offs)
+                    nc.sync.dma_start(gate_rows[0 : S // P, :], gate[0].rearrange("(c n) -> c n", n=P))
         w_raw = {}
         for i, w in enumerate((w1, w3)):
             w_rows = w.rearrange("(p j) c -> p j c", j=PACK)
-            for g in range(2):
-                w_raw[i, g] = keep.tile([P, PACK, H // 2], F32, name=f"w_raw{i}{g}")
-                nc.sync.dma_start(w_raw[i, g][:], w_rows[:, :, g * (H // 2) : (g + 1) * (H // 2)])
+            for g, (lo, hi) in enumerate(W_PIECES[i]):
+                w_raw[i, g] = keep.tile([P, PACK, hi - lo], F32, name=f"w_raw{i}{g}")
+                nc.sync.dma_start(w_raw[i, g][:], w_rows[:, :, lo:hi])
+        nc.sync.dma_start(w2_codes[:].bitcast(I32), w2_words[0].bitcast(I32))
+        for q in range(4):
+            nc.sync.dma_start(w2_plane[32 * q : 32 * q + 4, :].bitcast(I32), w2_scales[0, 4 * q : 4 * q + 4, :].bitcast(I32))
         window = keep.tile([P, T], F32, name="window")
         nc.sync.dma_start(window[:], res)
-        gate_sb = keep.tile([P, S], F32, name="gate_sb")
-        nc.sync.dma_start(gate_sb[:], gate)
-
-        w2_codes = keep.tile([P, 2 * N], U8, name="w2_codes", align_bytes=64)
-        w2_plane = keep.tile([P, N], U8, name="w2_plane", align_bytes=64)
-        nc.gpsimd.memset(w2_plane[:].bitcast(I32), 0)
-        nc.gpsimd.dma_start(w2_codes[:].bitcast(I32), w2_words[0].bitcast(I32))
-        for q in range(4):
-            nc.gpsimd.dma_start(w2_plane[32 * q : 32 * q + 4, :].bitcast(I32), w2_scales[0, 4 * q : 4 * q + 4, :].bitcast(I32))
 
         picked = [keep.tile([P, HALF, 2], U32, name=f"picked{g}", align_bytes=64) for g in range(2)]
         for u in range(2):
             pairs = keep.tile([P, T], U32, name=f"pairs{u}")
-            for q in range(pieces):
-                dst = pairs[:, q * PIECE : (q + 1) * PIECE].bitcast(BF16).rearrange("p (n j) -> p n j", j=2)
+            for q, (lo, hi) in enumerate(X_PIECES[u]):
+                dst = pairs[:, lo:hi].bitcast(BF16).rearrange("p (n j) -> p n j", j=2)
                 src = raw[u, q][:].rearrange("p j n -> p n j")
-                if u == 0 or q == pieces - 1:
+                if u == 0 or q >= 3:
                     nc.vector.tensor_copy(dst, src)
                 else:
                     nc.scalar.copy(dst, src)
             for g in range(2):
                 nc.vector.tensor_copy(picked[g][:, :, u], pairs[:].indirect(offsets[:, g * (HALF // 16) : (g + 1) * (HALF // 16)]))
 
-        x_codes = [keep.tile([P, HALF], U32, name=f"x_codes{g}", align_bytes=64) for g in range(2)]
-        x_plane = [keep.tile([P, HALF], U8, name=f"x_plane{g}", align_bytes=64) for g in range(2)]
-        for g in range(2):
-            nc.vector.quantize_mx(
-                out=x_codes[g][:].bitcast(FP8X4),
-                scales=x_plane[g][:],
-                in_=picked[g][:].rearrange("p n u -> p (n u)").bitcast(BF16),
-            )
+        x_codes, x_plane = [], []
 
+        def quantize_picked(g, tag):
+            codes = keep.tile([P, HALF], U32, name=f"x_codes{g}", tag=tag, align_bytes=64)
+            plane = keep.tile([P, HALF], U8, name=f"x_plane{g}", align_bytes=64)
+            nc.vector.quantize_mx(out=codes[:].bitcast(FP8X4), scales=plane[:], in_=picked[g][:].rearrange("p n u -> p (n u)").bitcast(BF16))
+            x_codes.append(codes)
+            x_plane.append(plane)
+
+        quantize_picked(0, "x_codes0")
         w_codes, w_plane = [], []
         for i in range(2):
-            grouped = keep.tile([P, PACK * H], BF16, name=f"w_grouped{i}", align_bytes=64)
-            for g in range(2):
-                dst = grouped[:].rearrange("p (t m j) -> p m t j", t=PACK, j=PACK)[:, g * 64 : (g + 1) * 64, :, :]
+            grouped = keep.tile([P, PACK * H], BF16, name=f"w_grouped{i}", tag=f"w_grouped{i}", align_bytes=64)
+            for g, (lo, hi) in enumerate(W_PIECES[i]):
+                dst = grouped[:].rearrange("p (t m j) -> p m t j", t=PACK, j=PACK)[:, lo // PACK : hi // PACK, :, :]
                 src = w_raw[i, g][:].rearrange("p j (m t) -> p m t j", t=PACK)
-                if (i, g) == (1, 1):
+                if i == 1 and g >= 1:
                     nc.vector.tensor_copy(dst, src)
                 else:
                     nc.scalar.copy(dst, src)
             codes = keep.tile([P, H], U32, name=f"w_codes{i}", align_bytes=64)
             plane = keep.tile([P, H], U8, name=f"w_plane{i}", align_bytes=64)
-            nc.vector.quantize_mx(out=codes[:].bitcast(FP8X4), scales=plane[:], in_=grouped[:])
+            for g in range(2):
+                cols = slice(g * (H // 2), (g + 1) * (H // 2))
+                nc.vector.quantize_mx(out=codes[:, cols].bitcast(FP8X4), scales=plane[:, cols], in_=grouped[:, g * 2 * H : (g + 1) * 2 * H])
             w_codes.append(codes)
             w_plane.append(plane)
+
+        quantize_picked(1, "w_grouped1")
 
         def up(i, g, c):
             acc = psum_up.tile([P, PACK, CHUNK], F32, name=f"up{i}")
@@ -111,35 +125,61 @@ def tile_picked_modres_glusilu_l_kernel(tc, xT, gate, res, w1, w3, w2_words, w2_
                 )
             return acc[:].rearrange("p t n -> p n t")
 
-        gated = []
-        for g in range(2):
-            hidden = keep.tile([P, HALF, PACK], BF16, name=f"hidden{g}", align_bytes=64)
-            for c in range(HALF // CHUNK):
-                act = keep.tile([P, CHUNK, PACK], F32, name=f"act{g}{c}")
-                nc.scalar.activation(act[:], up(0, g, c), ACT.Silu)
-                nc.vector.tensor_tensor(hidden[:, c * CHUNK : (c + 1) * CHUNK, :], up(1, g, c), act[:], ALU.mult)
-            h_codes = keep.tile([P, HALF], U32, name=f"h_codes{g}", align_bytes=64)
-            h_plane = keep.tile([P, HALF], U8, name=f"h_plane{g}", align_bytes=64)
-            nc.vector.quantize_mx(out=h_codes[:].bitcast(FP8X4), scales=h_plane[:], in_=hidden[:].rearrange("p n t -> p (n t)"))
-            y = psum_down.tile([P, HALF], F32, name="y")
-            nc.tensor.matmul_mx(
-                out=y[:],
-                lhsT=w2_codes[:].bitcast(FP4X4),
-                lhsT_scale=w2_plane[:],
-                rhs=h_codes[:].bitcast(FP8X4),
-                rhs_scale=h_plane[:],
-                start=True,
-                stop=True,
-            )
-            gated.append(y)
+        hidden = [keep.tile([P, HALF, PACK], BF16, name=f"hidden{g}", align_bytes=64) for g in range(2)]
+        h_codes = [keep.tile([P, HALF], U32, name=f"h_codes{g}", align_bytes=64) for g in range(2)]
+        h_plane = [keep.tile([P, HALF], U8, name=f"h_plane{g}", align_bytes=64) for g in range(2)]
+        old = [keep.tile([P, HALF], F32, name=f"old{g}") for g in range(2)]
+        update = [keep.tile([P, HALF], F32, name=f"update{g}") for g in range(2)]
+        chunks = HALF // CHUNK
 
-        old = keep.tile([P, S], F32, name="old")
-        nc.vector.tensor_copy(old[:], window[:].indirect(offsets[:]))
+        def entries(g):
+            return offsets[:, g * (HALF // 16) : (g + 1) * (HALF // 16)]
+
+        def gated_chunk(g, c):
+            act = keep.tile([P, CHUNK, PACK], F32, name=f"act{g}{c}")
+            nc.scalar.activation(act[:], up(0, g, c), ACT.Silu)
+            nc.vector.tensor_tensor(hidden[g][:, c * CHUNK : (c + 1) * CHUNK, :], up(1, g, c), act[:], ALU.mult)
+
+        def quantize_hidden(g):
+            nc.vector.quantize_mx(out=h_codes[g][:].bitcast(FP8X4), scales=h_plane[g][:], in_=hidden[g][:].rearrange("p n t -> p (n t)"))
+
+        def down(g):
+            y_rows = psum_down.tile([P, chunks, N], F32, name="y_rows")
+            for c in range(chunks):
+                cols = slice(c * CHUNK, (c + 1) * CHUNK)
+                nc.tensor.matmul_mx(
+                    out=y_rows[:, c, :],
+                    lhsT=h_codes[g][:, cols].bitcast(FP8X4),
+                    lhsT_scale=h_plane[g][:, cols],
+                    rhs=w2_codes[:].bitcast(FP4X4),
+                    rhs_scale=w2_plane[:],
+                    start=True,
+                    stop=True,
+                )
+            scaled = keep.tile([P, chunks, N], F32, name=f"scaled{g}")
+            for c in range(chunks):
+                nc.scalar.activation(scaled[:, c, :], y_rows[:, c, :], ACT.Copy, scale=gate_cols[:, g * chunks + c : g * chunks + c + 1])
+            turned = psum_down.tile([P, chunks, CHUNK], F32, name="turned")
+            for c in range(chunks):
+                nc.tensor.transpose(turned[:, c, :], scaled[:, c, :], identity[:])
+            nc.scalar.copy(update[g][:], turned[:].rearrange("p c n -> p (c n)"))
+
+        gate_cols = keep.tile([P, S // P], F32, name="gate_cols")
+        gate_turned = psum_down.tile([P, chunks, CHUNK], F32, name="turned")
+        nc.tensor.transpose(gate_turned[:, 0, :], gate_rows[:], identity[:])
+        nc.scalar.copy(gate_cols[:], gate_turned[:, 0, 0 : S // P])
+
+        for c in range(chunks):
+            gated_chunk(0, c)
+        gated_chunk(1, 0)
+        quantize_hidden(0)
+        for c in range(1, chunks):
+            gated_chunk(1, c)
+        down(0)
+        nc.vector.tensor_copy(old[0][:], window[:].indirect(entries(0)))
+        quantize_hidden(1)
+        down(1)
+        nc.vector.tensor_copy(old[1][:], window[:].indirect(entries(1)))
         for g in range(2):
-            cols = slice(g * HALF, (g + 1) * HALF)
-            update = keep.tile([P, HALF], F32, name=f"update{g}")
-            nc.vector.tensor_tensor(update[:], gated[g][:], gate_sb[:, cols], ALU.mult)
-            nc.vector.tensor_tensor(
-                window[:].indirect(offsets[:, g * (HALF // 16) : (g + 1) * (HALF // 16)]), old[:, cols], update[:], ALU.add
-            )
+            nc.vector.tensor_tensor(window[:].indirect(entries(g)), old[g][:], update[g][:], ALU.add)
         nc.sync.dma_start(out, window[:])

@@ -19,10 +19,8 @@ ACT = mybir.ActivationFunctionType
 
 P = 128
 PACK = 4
-X_PIECES = (
-    ((0, 1024), (1024, 1536), (1536, 1792), (1792, 2048)),
-    ((0, 512), (512, 1024), (1024, 1536), (1536, 1792), (1792, 2048)),
-)
+X_PIECES = (((0, 1024), (1024, 1536), (1536, 2048)), ((0, 1024), (1024, 1536), (1536, 1792), (1792, 2048)))
+X_SCALAR = ((0, 0, 176), (1024, 0, 0, 96))
 W_PIECES = (((0, 256), (256, 512)), ((0, 256), (256, 384), (384, 512)))
 HALF = S // 2
 CHUNK = 128
@@ -73,10 +71,11 @@ def tile_picked_modres_glusilu_l_kernel(tc, xT, gate, res, w1, w3, w2_words, w2_
             for q, (lo, hi) in enumerate(X_PIECES[u]):
                 dst = pairs[:, lo:hi].bitcast(BF16).rearrange("p (n j) -> p n j", j=2)
                 src = raw[u, q][:].rearrange("p j n -> p n j")
-                if u == 0 or q >= 3:
-                    nc.vector.tensor_copy(dst, src)
-                else:
-                    nc.scalar.copy(dst, src)
+                share = X_SCALAR[u][q]
+                if share > 0:
+                    nc.scalar.copy(dst[:, :share, :], src[:, :share, :])
+                if share < hi - lo:
+                    nc.vector.tensor_copy(dst[:, share:, :], src[:, share:, :])
             for g in range(2):
                 nc.vector.tensor_copy(picked[g][:, :, u], pairs[:].indirect(offsets[:, g * (HALF // 16) : (g + 1) * (HALF // 16)]))
 
@@ -128,7 +127,7 @@ def tile_picked_modres_glusilu_l_kernel(tc, xT, gate, res, w1, w3, w2_words, w2_
         hidden = [keep.tile([P, HALF, PACK], BF16, name=f"hidden{g}", align_bytes=64) for g in range(2)]
         h_codes = [keep.tile([P, HALF], U32, name=f"h_codes{g}", align_bytes=64) for g in range(2)]
         h_plane = [keep.tile([P, HALF], U8, name=f"h_plane{g}", align_bytes=64) for g in range(2)]
-        old = [keep.tile([P, HALF], F32, name=f"old{g}") for g in range(2)]
+        old = [keep.tile([P, HALF], F32, name="old0")]
         update = [keep.tile([P, HALF], F32, name=f"update{g}") for g in range(2)]
         chunks = HALF // CHUNK
 
@@ -138,7 +137,13 @@ def tile_picked_modres_glusilu_l_kernel(tc, xT, gate, res, w1, w3, w2_words, w2_
         def gated_chunk(g, c):
             act = keep.tile([P, CHUNK, PACK], F32, name=f"act{g}{c}")
             nc.scalar.activation(act[:], up(0, g, c), ACT.Silu)
-            nc.vector.tensor_tensor(hidden[g][:, c * CHUNK : (c + 1) * CHUNK, :], up(1, g, c), act[:], ALU.mult)
+            dst = hidden[g][:, c * CHUNK : (c + 1) * CHUNK, :]
+            if g == 1 and c >= 2:
+                lin = keep.tile([P, CHUNK, PACK], F32, name=f"lin{c}")
+                nc.scalar.copy(lin[:], up(1, g, c))
+                nc.gpsimd.tensor_tensor(dst, lin[:], act[:], ALU.mult)
+            else:
+                nc.vector.tensor_tensor(dst, up(1, g, c), act[:], ALU.mult)
 
         def quantize_hidden(g):
             nc.vector.quantize_mx(out=h_codes[g][:].bitcast(FP8X4), scales=h_plane[g][:], in_=hidden[g][:].rearrange("p n t -> p (n t)"))
@@ -179,6 +184,7 @@ def tile_picked_modres_glusilu_l_kernel(tc, xT, gate, res, w1, w3, w2_words, w2_
         nc.vector.tensor_copy(old[0][:], window[:].indirect(entries(0)))
         quantize_hidden(1)
         down(1)
+        old.append(keep.tile([P, HALF], F32, name="old1"))
         nc.vector.tensor_copy(old[1][:], window[:].indirect(entries(1)))
         for g in range(2):
             nc.vector.tensor_tensor(window[:].indirect(entries(g)), old[g][:], update[g][:], ALU.add)

@@ -19,18 +19,25 @@ ACT = mybir.ActivationFunctionType
 
 P = 128
 PACK = 4
-X_PIECES = (((0, 1024), (1024, 1536), (1536, 2048)), ((0, 1024), (1024, 1536), (1536, 1792), (1792, 2048)))
-X_SCALAR = ((0, 0, 176), (1024, 0, 0, 96))
-W_PIECES = (((0, 256), (256, 512)), ((0, 256), (256, 384), (384, 512)))
 HALF = S // 2
 CHUNK = 128
+CHUNKS = HALF // CHUNK
+
+X_PIECES = (((0, 1024), (1024, 1536), (1536, 2048)), ((0, 1024), (1024, 1536), (1536, 1792), (1792, 2048)))
+X_SCALAR = ((0, 0, 176), (1024, 0, 0, 96))
+W_PIECES = (
+    ((0, 256, "scalar"), (256, 512, "gpsimd")),
+    ((0, 256, "scalar"), (256, 384, "vector"), (384, 512, "vector")),
+)
+GPSIMD_CHUNKS = ((0, 1), (1, 0), (1, 2))
+UP_BANKS = 3
 
 
 def tile_picked_modres_glusilu_l_kernel(tc, xT, gate, res, w1, w3, w2_words, w2_scales, offs, out):
     nc = tc.nc
     with ExitStack() as ctx:
         keep = ctx.enter_context(tc.tile_pool(name="keep", bufs=1))
-        psum_up = ctx.enter_context(tc.psum_pool(name="psum_up", bufs=3))
+        psum_up = ctx.enter_context(tc.psum_pool(name="psum_up", bufs=UP_BANKS))
         psum_down = ctx.enter_context(tc.psum_pool(name="psum_down", bufs=1))
 
         offsets = keep.tile([P, S // 16], U16, name="offsets")
@@ -39,12 +46,15 @@ def tile_picked_modres_glusilu_l_kernel(tc, xT, gate, res, w1, w3, w2_words, w2_
         w2_plane = keep.tile([P, N], U8, name="w2_plane", align_bytes=64)
         gate_rows = keep.tile([P, P], F32, name="gate_rows")
         identity = keep.tile([P, P], F32, name="identity")
+
         warm = keep.tile([P, 2], F32, name="warm")
         nc.gpsimd.memset(warm[:, 0:1], 0.0)
         nc.scalar.activation(warm[:, 1:2], warm[:, 0:1], ACT.Silu)
+
         nc.gpsimd.memset(w2_plane[:].bitcast(I32), 0)
         nc.gpsimd.memset(gate_rows[:], 0.0)
         make_identity(nc, identity[:])
+
         raw = {}
         for u in range(2):
             for q, (lo, hi) in enumerate(X_PIECES[u]):
@@ -56,14 +66,20 @@ def tile_picked_modres_glusilu_l_kernel(tc, xT, gate, res, w1, w3, w2_words, w2_
         w_raw = {}
         for i, w in enumerate((w1, w3)):
             w_rows = w.rearrange("(p j) c -> p j c", j=PACK)
-            for g, (lo, hi) in enumerate(W_PIECES[i]):
-                w_raw[i, g] = keep.tile([P, PACK, hi - lo], F32, name=f"w_raw{i}{g}")
-                nc.sync.dma_start(w_raw[i, g][:], w_rows[:, :, lo:hi])
+            for q, (lo, hi, engine) in enumerate(W_PIECES[i]):
+                w_raw[i, q] = keep.tile([P, PACK, hi - lo], F32, name=f"w_raw{i}{q}")
+                nc.sync.dma_start(w_raw[i, q][:], w_rows[:, :, lo:hi])
         nc.sync.dma_start(w2_codes[:].bitcast(I32), w2_words[0].bitcast(I32))
-        for q in range(4):
-            nc.sync.dma_start(w2_plane[32 * q : 32 * q + 4, :].bitcast(I32), w2_scales[0, 4 * q : 4 * q + 4, :].bitcast(I32))
+        for quadrant in range(4):
+            nc.sync.dma_start(
+                w2_plane[32 * quadrant : 32 * quadrant + 4, :].bitcast(I32),
+                w2_scales[0, 4 * quadrant : 4 * quadrant + 4, :].bitcast(I32),
+            )
         window = keep.tile([P, T], F32, name="window")
         nc.sync.dma_start(window[:], res)
+
+        def entries(g):
+            return offsets[:, g * (HALF // 16) : (g + 1) * (HALF // 16)]
 
         picked = [keep.tile([P, HALF, 2], U32, name=f"picked{g}", align_bytes=64) for g in range(2)]
         for u in range(2):
@@ -77,33 +93,43 @@ def tile_picked_modres_glusilu_l_kernel(tc, xT, gate, res, w1, w3, w2_words, w2_
                 if share < hi - lo:
                     nc.vector.tensor_copy(dst[:, share:, :], src[:, share:, :])
             for g in range(2):
-                nc.vector.tensor_copy(picked[g][:, :, u], pairs[:].indirect(offsets[:, g * (HALF // 16) : (g + 1) * (HALF // 16)]))
+                nc.vector.tensor_copy(picked[g][:, :, u], pairs[:].indirect(entries(g)))
 
         x_codes, x_plane = [], []
 
         def quantize_picked(g, tag):
             codes = keep.tile([P, HALF], U32, name=f"x_codes{g}", tag=tag, align_bytes=64)
             plane = keep.tile([P, HALF], U8, name=f"x_plane{g}", align_bytes=64)
-            nc.vector.quantize_mx(out=codes[:].bitcast(FP8X4), scales=plane[:], in_=picked[g][:].rearrange("p n u -> p (n u)").bitcast(BF16))
+            nc.vector.quantize_mx(
+                out=codes[:].bitcast(FP8X4),
+                scales=plane[:],
+                in_=picked[g][:].rearrange("p n u -> p (n u)").bitcast(BF16),
+            )
             x_codes.append(codes)
             x_plane.append(plane)
 
         quantize_picked(0, "x_codes0")
+
         w_codes, w_plane = [], []
         for i in range(2):
             grouped = keep.tile([P, PACK * H], BF16, name=f"w_grouped{i}", tag=f"w_grouped{i}", align_bytes=64)
-            for g, (lo, hi) in enumerate(W_PIECES[i]):
+            for q, (lo, hi, engine) in enumerate(W_PIECES[i]):
                 dst = grouped[:].rearrange("p (t m j) -> p m t j", t=PACK, j=PACK)[:, lo // PACK : hi // PACK, :, :]
-                src = w_raw[i, g][:].rearrange("p j (m t) -> p m t j", t=PACK)
-                if i == 1 and g >= 1:
+                src = w_raw[i, q][:].rearrange("p j (m t) -> p m t j", t=PACK)
+                if engine == "vector":
                     nc.vector.tensor_copy(dst, src)
+                elif engine == "gpsimd":
+                    nc.gpsimd.tensor_scalar(dst, src, 1.0, 0.0, ALU.mult, ALU.add)
                 else:
                     nc.scalar.copy(dst, src)
             codes = keep.tile([P, H], U32, name=f"w_codes{i}", align_bytes=64)
             plane = keep.tile([P, H], U8, name=f"w_plane{i}", align_bytes=64)
-            for g in range(2):
-                cols = slice(g * (H // 2), (g + 1) * (H // 2))
-                nc.vector.quantize_mx(out=codes[:, cols].bitcast(FP8X4), scales=plane[:, cols], in_=grouped[:, g * 2 * H : (g + 1) * 2 * H])
+            for side in range(2):
+                nc.vector.quantize_mx(
+                    out=codes[:, side * (H // 2) : (side + 1) * (H // 2)].bitcast(FP8X4),
+                    scales=plane[:, side * (H // 2) : (side + 1) * (H // 2)],
+                    in_=grouped[:, side * 2 * H : (side + 1) * 2 * H],
+                )
             w_codes.append(codes)
             w_plane.append(plane)
 
@@ -127,30 +153,28 @@ def tile_picked_modres_glusilu_l_kernel(tc, xT, gate, res, w1, w3, w2_words, w2_
         hidden = [keep.tile([P, HALF, PACK], BF16, name=f"hidden{g}", align_bytes=64) for g in range(2)]
         h_codes = [keep.tile([P, HALF], U32, name=f"h_codes{g}", align_bytes=64) for g in range(2)]
         h_plane = [keep.tile([P, HALF], U8, name=f"h_plane{g}", align_bytes=64) for g in range(2)]
-        old = [keep.tile([P, HALF], F32, name="old0")]
+        old = [keep.tile([P, HALF], F32, name=f"old{g}") for g in range(2)]
         update = [keep.tile([P, HALF], F32, name=f"update{g}") for g in range(2)]
-        chunks = HALF // CHUNK
-
-        def entries(g):
-            return offsets[:, g * (HALF // 16) : (g + 1) * (HALF // 16)]
 
         def gated_chunk(g, c):
             act = keep.tile([P, CHUNK, PACK], F32, name=f"act{g}{c}")
             nc.scalar.activation(act[:], up(0, g, c), ACT.Silu)
             dst = hidden[g][:, c * CHUNK : (c + 1) * CHUNK, :]
-            if g == 1 and c >= 2:
-                lin = keep.tile([P, CHUNK, PACK], F32, name=f"lin{c}")
+            if (g, c) in GPSIMD_CHUNKS:
+                lin = keep.tile([P, CHUNK, PACK], F32, name=f"lin{g}{c}")
                 nc.scalar.copy(lin[:], up(1, g, c))
                 nc.gpsimd.tensor_tensor(dst, lin[:], act[:], ALU.mult)
             else:
                 nc.vector.tensor_tensor(dst, up(1, g, c), act[:], ALU.mult)
 
         def quantize_hidden(g):
-            nc.vector.quantize_mx(out=h_codes[g][:].bitcast(FP8X4), scales=h_plane[g][:], in_=hidden[g][:].rearrange("p n t -> p (n t)"))
+            nc.vector.quantize_mx(
+                out=h_codes[g][:].bitcast(FP8X4), scales=h_plane[g][:], in_=hidden[g][:].rearrange("p n t -> p (n t)")
+            )
 
         def down(g):
-            y_rows = psum_down.tile([P, chunks, N], F32, name="y_rows")
-            for c in range(chunks):
+            y_rows = psum_down.tile([P, CHUNKS, N], F32, name="y_rows")
+            for c in range(CHUNKS):
                 cols = slice(c * CHUNK, (c + 1) * CHUNK)
                 nc.tensor.matmul_mx(
                     out=y_rows[:, c, :],
@@ -161,31 +185,32 @@ def tile_picked_modres_glusilu_l_kernel(tc, xT, gate, res, w1, w3, w2_words, w2_
                     start=True,
                     stop=True,
                 )
-            scaled = keep.tile([P, chunks, N], F32, name=f"scaled{g}")
-            for c in range(chunks):
-                nc.scalar.activation(scaled[:, c, :], y_rows[:, c, :], ACT.Copy, scale=gate_cols[:, g * chunks + c : g * chunks + c + 1])
-            turned = psum_down.tile([P, chunks, CHUNK], F32, name="turned")
-            for c in range(chunks):
+            scaled = keep.tile([P, CHUNKS, N], F32, name=f"scaled{g}")
+            for c in range(CHUNKS):
+                column = g * CHUNKS + c
+                nc.scalar.activation(scaled[:, c, :], y_rows[:, c, :], ACT.Copy, scale=gate_cols[:, column : column + 1])
+            turned = psum_down.tile([P, CHUNKS, CHUNK], F32, name="turned")
+            for c in range(CHUNKS):
                 nc.tensor.transpose(turned[:, c, :], scaled[:, c, :], identity[:])
             nc.scalar.copy(update[g][:], turned[:].rearrange("p c n -> p (c n)"))
 
         gate_cols = keep.tile([P, S // P], F32, name="gate_cols")
-        gate_turned = psum_down.tile([P, chunks, CHUNK], F32, name="turned")
+        gate_turned = psum_down.tile([P, CHUNKS, CHUNK], F32, name="turned")
         nc.tensor.transpose(gate_turned[:, 0, :], gate_rows[:], identity[:])
         nc.scalar.copy(gate_cols[:], gate_turned[:, 0, 0 : S // P])
 
-        for c in range(chunks):
+        for c in range(CHUNKS):
             gated_chunk(0, c)
         gated_chunk(1, 0)
         quantize_hidden(0)
-        for c in range(1, chunks):
+        for c in range(1, CHUNKS):
             gated_chunk(1, c)
         down(0)
         nc.vector.tensor_copy(old[0][:], window[:].indirect(entries(0)))
         quantize_hidden(1)
         down(1)
-        old.append(keep.tile([P, HALF], F32, name="old1"))
         nc.vector.tensor_copy(old[1][:], window[:].indirect(entries(1)))
+
         for g in range(2):
             nc.vector.tensor_tensor(window[:].indirect(entries(g)), old[g][:], update[g][:], ALU.add)
         nc.sync.dma_start(out, window[:])

@@ -26,10 +26,11 @@ CHUNKS = HALF // CHUNK
 X_PIECES = (((0, 1024), (1024, 1536), (1536, 2048)), ((0, 1024), (1024, 1536), (1536, 1792), (1792, 2048)))
 X_SCALAR = ((0, 0, 176), (1024, 0, 0, 96))
 W_PIECES = (
-    ((0, 256, "scalar"), (256, 512, "gpsimd")),
+    ((0, 256, "scalar"), (256, 512, "scalar")),
     ((0, 256, "scalar"), (256, 384, "vector"), (384, 512, "vector")),
 )
 GPSIMD_CHUNKS = ((0, 1), (1, 0), (1, 2))
+LOOSE_PIECES = (((0, HALF),), ((0, HALF // 2), (HALF // 2, HALF)))
 UP_BANKS = 3
 
 
@@ -82,6 +83,7 @@ def tile_picked_modres_glusilu_l_kernel(tc, xT, gate, res, w1, w3, w2_words, w2_
             return offsets[:, g * (HALF // 16) : (g + 1) * (HALF // 16)]
 
         picked = [keep.tile([P, HALF, 2], U32, name=f"picked{g}", align_bytes=64) for g in range(2)]
+        loose = keep.tile([P, 2, HALF], U32, name="loose")
         for u in range(2):
             pairs = keep.tile([P, T], U32, name=f"pairs{u}")
             for q, (lo, hi) in enumerate(X_PIECES[u]):
@@ -92,8 +94,11 @@ def tile_picked_modres_glusilu_l_kernel(tc, xT, gate, res, w1, w3, w2_words, w2_
                     nc.scalar.copy(dst[:, :share, :], src[:, :share, :])
                 if share < hi - lo:
                     nc.vector.tensor_copy(dst[:, share:, :], src[:, share:, :])
-            for g in range(2):
-                nc.vector.tensor_copy(picked[g][:, :, u], pairs[:].indirect(entries(g)))
+            for lo, hi in LOOSE_PIECES[u]:
+                nc.vector.tensor_copy(loose[:, u, lo:hi], pairs[:].indirect(offsets[:, lo // 16 : hi // 16]))
+                if u == 1:
+                    nc.gpsimd.tensor_copy(picked[0][:, lo:hi, :], loose[:, :, lo:hi].rearrange("p u n -> p n u"))
+            nc.vector.tensor_copy(picked[1][:, :, u], pairs[:].indirect(entries(1)))
 
         x_codes, x_plane = [], []
 

@@ -26,11 +26,15 @@ CHUNKS = HALF // CHUNK
 X_PIECES = (((0, 1024), (1024, 1536), (1536, 2048)), ((0, 1024), (1024, 1536), (1536, 1792), (1792, 2048)))
 X_SCALAR = ((0, 0, 176), (1024, 0, 0, 96))
 W_PIECES = (
-    ((0, 256, "scalar"), (256, 512, "scalar")),
-    ((0, 256, "scalar"), (256, 384, "vector"), (384, 512, "vector")),
+    ((0, 256, ((0, 256, "scalar"),)), (256, 512, ((256, 336, "gpsimd"), (336, 512, "scalar")))),
+    (
+        (0, 256, ((0, 256, "scalar"),)),
+        (256, 384, ((256, 384, "vector"),)),
+        (384, 512, ((384, 512, "vector"),)),
+    ),
 )
 GPSIMD_CHUNKS = ((0, 1), (1, 0), (1, 2))
-LOOSE_PIECES = (((0, HALF),), ((0, HALF // 2), (HALF // 2, HALF)))
+LOOSE_RUNS = (((0, HALF),), ((0, HALF // 2), (HALF // 2, HALF)))
 UP_BANKS = 3
 
 
@@ -67,7 +71,7 @@ def tile_picked_modres_glusilu_l_kernel(tc, xT, gate, res, w1, w3, w2_words, w2_
         w_raw = {}
         for i, w in enumerate((w1, w3)):
             w_rows = w.rearrange("(p j) c -> p j c", j=PACK)
-            for q, (lo, hi, engine) in enumerate(W_PIECES[i]):
+            for q, (lo, hi, shares) in enumerate(W_PIECES[i]):
                 w_raw[i, q] = keep.tile([P, PACK, hi - lo], F32, name=f"w_raw{i}{q}")
                 nc.sync.dma_start(w_raw[i, q][:], w_rows[:, :, lo:hi])
         nc.sync.dma_start(w2_codes[:].bitcast(I32), w2_words[0].bitcast(I32))
@@ -94,7 +98,7 @@ def tile_picked_modres_glusilu_l_kernel(tc, xT, gate, res, w1, w3, w2_words, w2_
                     nc.scalar.copy(dst[:, :share, :], src[:, :share, :])
                 if share < hi - lo:
                     nc.vector.tensor_copy(dst[:, share:, :], src[:, share:, :])
-            for lo, hi in LOOSE_PIECES[u]:
+            for lo, hi in LOOSE_RUNS[u]:
                 nc.vector.tensor_copy(loose[:, u, lo:hi], pairs[:].indirect(offsets[:, lo // 16 : hi // 16]))
                 if u == 1:
                     nc.gpsimd.tensor_copy(picked[0][:, lo:hi, :], loose[:, :, lo:hi].rearrange("p u n -> p n u"))
@@ -118,15 +122,16 @@ def tile_picked_modres_glusilu_l_kernel(tc, xT, gate, res, w1, w3, w2_words, w2_
         w_codes, w_plane = [], []
         for i in range(2):
             grouped = keep.tile([P, PACK * H], BF16, name=f"w_grouped{i}", tag=f"w_grouped{i}", align_bytes=64)
-            for q, (lo, hi, engine) in enumerate(W_PIECES[i]):
-                dst = grouped[:].rearrange("p (t m j) -> p m t j", t=PACK, j=PACK)[:, lo // PACK : hi // PACK, :, :]
-                src = w_raw[i, q][:].rearrange("p j (m t) -> p m t j", t=PACK)
-                if engine == "vector":
-                    nc.vector.tensor_copy(dst, src)
-                elif engine == "gpsimd":
-                    nc.gpsimd.tensor_scalar(dst, src, 1.0, 0.0, ALU.mult, ALU.add)
-                else:
-                    nc.scalar.copy(dst, src)
+            for q, (first, last, shares) in enumerate(W_PIECES[i]):
+                for lo, hi, engine in shares:
+                    dst = grouped[:].rearrange("p (t m j) -> p m t j", t=PACK, j=PACK)[:, lo // PACK : hi // PACK, :, :]
+                    src = w_raw[i, q][:, :, lo - first : hi - first].rearrange("p j (m t) -> p m t j", t=PACK)
+                    if engine == "vector":
+                        nc.vector.tensor_copy(dst, src)
+                    elif engine == "gpsimd":
+                        nc.gpsimd.tensor_scalar(dst, src, 1.0, 0.0, ALU.mult, ALU.add)
+                    else:
+                        nc.scalar.copy(dst, src)
             codes = keep.tile([P, H], U32, name=f"w_codes{i}", align_bytes=64)
             plane = keep.tile([P, H], U8, name=f"w_plane{i}", align_bytes=64)
             for side in range(2):

@@ -1,7 +1,6 @@
 from contextlib import ExitStack
 
 import concourse.mybir as mybir
-from concourse.masks import make_identity
 
 K, T, S, H, N = 512, 2048, 1024, 512, 128
 FLOPS = 2 * S * (2 * K * H + H * N)
@@ -29,12 +28,13 @@ W_PIECES = (
     ((0, 256, ((0, 256, "scalar"),)), (256, 512, ((256, 336, "gpsimd"), (336, 512, "scalar")))),
     (
         (0, 256, ((0, 256, "scalar"),)),
-        (256, 384, ((256, 384, "vector"),)),
-        (384, 512, ((384, 512, "vector"),)),
+        (256, 512, ((256, 512, "vector"),)),
     ),
 )
-GPSIMD_CHUNKS = ((0, 1), (1, 0), (1, 2))
+PIECES = ((0, 256, "scalar"), (256, 512, "scalar"), (512, 768, "scalar"), (768, 1024, "vector"))
 LOOSE_RUNS = (((0, HALF),), ((0, HALF // 2), (HALF // 2, HALF)))
+FETCH = ("vector", "scalar", "vector", "vector")
+SHARED = 256
 UP_BANKS = 3
 
 
@@ -43,22 +43,18 @@ def tile_picked_modres_glusilu_l_kernel(tc, xT, gate, res, w1, w3, w2_words, w2_
     with ExitStack() as ctx:
         keep = ctx.enter_context(tc.tile_pool(name="keep", bufs=1))
         psum_up = ctx.enter_context(tc.psum_pool(name="psum_up", bufs=UP_BANKS))
-        psum_down = ctx.enter_context(tc.psum_pool(name="psum_down", bufs=1))
+        psum_down = ctx.enter_context(tc.psum_pool(name="psum_down", bufs=2))
 
         offsets = keep.tile([P, S // 16], U16, name="offsets")
         x_rows = xT.rearrange("(p j) n -> p j n", j=PACK)
         w2_codes = keep.tile([P, 2 * N], U8, name="w2_codes", align_bytes=64)
         w2_plane = keep.tile([P, N], U8, name="w2_plane", align_bytes=64)
-        gate_rows = keep.tile([P, P], F32, name="gate_rows")
-        identity = keep.tile([P, P], F32, name="identity")
 
         warm = keep.tile([P, 2], F32, name="warm")
         nc.gpsimd.memset(warm[:, 0:1], 0.0)
         nc.scalar.activation(warm[:, 1:2], warm[:, 0:1], ACT.Silu)
 
         nc.gpsimd.memset(w2_plane[:].bitcast(I32), 0)
-        nc.gpsimd.memset(gate_rows[:], 0.0)
-        make_identity(nc, identity[:])
 
         raw = {}
         for u in range(2):
@@ -67,7 +63,6 @@ def tile_picked_modres_glusilu_l_kernel(tc, xT, gate, res, w1, w3, w2_words, w2_
                 nc.sync.dma_start(raw[u, q][:], x_rows[:, 2 * u : 2 * u + 2, lo:hi])
                 if (u, q) == (0, 0):
                     nc.sync.dma_start(offsets[:], offs)
-                    nc.sync.dma_start(gate_rows[0 : S // P, :], gate[0].rearrange("(c n) -> c n", n=P))
         w_raw = {}
         for i, w in enumerate((w1, w3)):
             w_rows = w.rearrange("(p j) c -> p j c", j=PACK)
@@ -80,6 +75,10 @@ def tile_picked_modres_glusilu_l_kernel(tc, xT, gate, res, w1, w3, w2_words, w2_
                 w2_plane[32 * quadrant : 32 * quadrant + 4, :].bitcast(I32),
                 w2_scales[0, 4 * quadrant : 4 * quadrant + 4, :].bitcast(I32),
             )
+        source = keep.tile([P, T], F32, name="source")
+        nc.sync.dma_start(source[:], res)
+        gates = keep.tile([P, S], F32, name="gates")
+        nc.sync.dma_start(gates[:], gate)
         window = keep.tile([P, T], F32, name="window")
         nc.sync.dma_start(window[:], res)
 
@@ -106,25 +105,26 @@ def tile_picked_modres_glusilu_l_kernel(tc, xT, gate, res, w1, w3, w2_words, w2_
 
         x_codes, x_plane = [], []
 
-        def quantize_picked(g, tag):
-            codes = keep.tile([P, HALF], U32, name=f"x_codes{g}", tag=tag, align_bytes=64)
+        def quantize_picked(g, codes):
             plane = keep.tile([P, HALF], U8, name=f"x_plane{g}", align_bytes=64)
             nc.vector.quantize_mx(
-                out=codes[:].bitcast(FP8X4),
+                out=codes.bitcast(FP8X4),
                 scales=plane[:],
                 in_=picked[g][:].rearrange("p n u -> p (n u)").bitcast(BF16),
             )
             x_codes.append(codes)
             x_plane.append(plane)
 
-        quantize_picked(0, "x_codes0")
+        first_codes = keep.tile([P, HALF], U32, name="x_codes0", align_bytes=64)
+        quantize_picked(0, first_codes[:])
 
+        both = keep.tile([P, 2 * PACK * H - SHARED], BF16, name="w_grouped", tag="w_grouped", align_bytes=64)
         w_codes, w_plane = [], []
         for i in range(2):
-            grouped = keep.tile([P, PACK * H], BF16, name=f"w_grouped{i}", tag=f"w_grouped{i}", align_bytes=64)
+            grouped = both[:, (1 - i) * (PACK * H - SHARED) : (1 - i) * (PACK * H - SHARED) + PACK * H]
             for q, (first, last, shares) in enumerate(W_PIECES[i]):
                 for lo, hi, engine in shares:
-                    dst = grouped[:].rearrange("p (t m j) -> p m t j", t=PACK, j=PACK)[:, lo // PACK : hi // PACK, :, :]
+                    dst = grouped.rearrange("p (t m j) -> p m t j", t=PACK, j=PACK)[:, lo // PACK : hi // PACK, :, :]
                     src = w_raw[i, q][:, :, lo - first : hi - first].rearrange("p j (m t) -> p m t j", t=PACK)
                     if engine == "vector":
                         nc.vector.tensor_copy(dst, src)
@@ -132,7 +132,7 @@ def tile_picked_modres_glusilu_l_kernel(tc, xT, gate, res, w1, w3, w2_words, w2_
                         nc.gpsimd.tensor_scalar(dst, src, 1.0, 0.0, ALU.mult, ALU.add)
                     else:
                         nc.scalar.copy(dst, src)
-            codes = keep.tile([P, H], U32, name=f"w_codes{i}", align_bytes=64)
+            codes = keep.tile([P, H], U32, name=f"w_codes{i}", tag=f"w_codes{i}", align_bytes=64)
             plane = keep.tile([P, H], U8, name=f"w_plane{i}", align_bytes=64)
             for side in range(2):
                 nc.vector.quantize_mx(
@@ -143,7 +143,8 @@ def tile_picked_modres_glusilu_l_kernel(tc, xT, gate, res, w1, w3, w2_words, w2_
             w_codes.append(codes)
             w_plane.append(plane)
 
-        quantize_picked(1, "w_grouped1")
+        second_codes = keep.tile([P, HALF], U32, name="x_codes1", tag="w_grouped", align_bytes=64)
+        quantize_picked(1, second_codes[:])
 
         def up(i, g, c):
             acc = psum_up.tile([P, PACK, CHUNK], F32, name=f"up{i}")
@@ -160,67 +161,87 @@ def tile_picked_modres_glusilu_l_kernel(tc, xT, gate, res, w1, w3, w2_words, w2_
                 )
             return acc[:].rearrange("p t n -> p n t")
 
-        hidden = [keep.tile([P, HALF, PACK], BF16, name=f"hidden{g}", align_bytes=64) for g in range(2)]
-        h_codes = [keep.tile([P, HALF], U32, name=f"h_codes{g}", align_bytes=64) for g in range(2)]
-        h_plane = [keep.tile([P, HALF], U8, name=f"h_plane{g}", align_bytes=64) for g in range(2)]
-        old = [keep.tile([P, HALF], F32, name=f"old{g}") for g in range(2)]
-        update = [keep.tile([P, HALF], F32, name=f"update{g}") for g in range(2)]
+        old = {}
+        act = {}
 
-        def gated_chunk(g, c):
-            act = keep.tile([P, CHUNK, PACK], F32, name=f"act{g}{c}")
-            nc.scalar.activation(act[:], up(0, g, c), ACT.Silu)
-            dst = hidden[g][:, c * CHUNK : (c + 1) * CHUNK, :]
-            if (g, c) in GPSIMD_CHUNKS:
-                lin = keep.tile([P, CHUNK, PACK], F32, name=f"lin{g}{c}")
-                nc.scalar.copy(lin[:], up(1, g, c))
-                nc.gpsimd.tensor_tensor(dst, lin[:], act[:], ALU.mult)
-            else:
-                nc.vector.tensor_tensor(dst, up(1, g, c), act[:], ALU.mult)
+        def silu(g, c):
+            act[g, c] = keep.tile([P, CHUNK, PACK], F32, name=f"act{g}{c}", tag=f"act{g}{c}", align_bytes=64)
+            nc.scalar.activation(act[g, c][:], up(0, g, c), ACT.Silu)
 
-        def quantize_hidden(g):
+        for c in range(CHUNKS):
+            silu(0, c)
+        hidden = [keep.tile([P, hi - lo, PACK], BF16, name=f"hidden{lo}", align_bytes=64) for lo, hi, engine in PIECES]
+
+        def gated(k, first):
+            lo, hi, engine = PIECES[k]
+            g, c = divmod(first // CHUNK, CHUNKS)
+            nc.vector.tensor_tensor(hidden[k][:, first - lo : first - lo + CHUNK, :], up(1, g, c), act[g, c][:], ALU.mult)
+            if g == 0:
+                silu(1, c)
+
+        y = {}
+
+        def down(k):
+            lo, hi, engine = PIECES[k]
+            codes = keep.tile([P, hi - lo], U32, name=f"h_codes{k}", align_bytes=64)
+            plane = keep.tile([P, hi - lo], U8, name=f"h_plane{k}", align_bytes=64)
             nc.vector.quantize_mx(
-                out=h_codes[g][:].bitcast(FP8X4), scales=h_plane[g][:], in_=hidden[g][:].rearrange("p n t -> p (n t)")
+                out=codes[:].bitcast(FP8X4), scales=plane[:], in_=hidden[k][:].rearrange("p n t -> p (n t)")
             )
-
-        def down(g):
-            y_rows = psum_down.tile([P, CHUNKS, N], F32, name="y_rows")
-            for c in range(CHUNKS):
-                cols = slice(c * CHUNK, (c + 1) * CHUNK)
+            y[k] = psum_down.tile([P, hi - lo], F32, name="y")
+            for first in range(0, hi - lo, 256):
+                cols = slice(first, min(first + 256, hi - lo))
                 nc.tensor.matmul_mx(
-                    out=y_rows[:, c, :],
-                    lhsT=h_codes[g][:, cols].bitcast(FP8X4),
-                    lhsT_scale=h_plane[g][:, cols],
-                    rhs=w2_codes[:].bitcast(FP4X4),
-                    rhs_scale=w2_plane[:],
+                    out=y[k][:, cols],
+                    lhsT=w2_codes[:].bitcast(FP4X4),
+                    lhsT_scale=w2_plane[:],
+                    rhs=codes[:, cols].bitcast(FP8X4),
+                    rhs_scale=plane[:, cols],
                     start=True,
                     stop=True,
                 )
-            scaled = keep.tile([P, CHUNKS, N], F32, name=f"scaled{g}")
-            for c in range(CHUNKS):
-                column = g * CHUNKS + c
-                nc.scalar.activation(scaled[:, c, :], y_rows[:, c, :], ACT.Copy, scale=gate_cols[:, column : column + 1])
-            turned = psum_down.tile([P, CHUNKS, CHUNK], F32, name="turned")
-            for c in range(CHUNKS):
-                nc.tensor.transpose(turned[:, c, :], scaled[:, c, :], identity[:])
-            nc.scalar.copy(update[g][:], turned[:].rearrange("p c n -> p (c n)"))
 
-        gate_cols = keep.tile([P, S // P], F32, name="gate_cols")
-        gate_turned = psum_down.tile([P, CHUNKS, CHUNK], F32, name="turned")
-        nc.tensor.transpose(gate_turned[:, 0, :], gate_rows[:], identity[:])
-        nc.scalar.copy(gate_cols[:], gate_turned[:, 0, 0 : S // P])
+        update = {}
 
-        for c in range(CHUNKS):
-            gated_chunk(0, c)
-        gated_chunk(1, 0)
-        quantize_hidden(0)
-        for c in range(1, CHUNKS):
-            gated_chunk(1, c)
-        down(0)
-        nc.vector.tensor_copy(old[0][:], window[:].indirect(entries(0)))
-        quantize_hidden(1)
-        down(1)
-        nc.vector.tensor_copy(old[1][:], window[:].indirect(entries(1)))
+        def weigh(k):
+            lo, hi, engine = PIECES[k]
+            update[k] = keep.tile([P, hi - lo], F32, name=f"update{k}")
+            nc.vector.tensor_tensor(update[k][:], y[k][:], gates[:, lo:hi], ALU.mult)
 
-        for g in range(2):
-            nc.vector.tensor_tensor(window[:].indirect(entries(g)), old[g][:], update[g][:], ALU.add)
+        def put(k):
+            lo, hi, engine = PIECES[k]
+            places = window[:].indirect(offsets[:, lo // 16 : hi // 16])
+            before = old[k][:]
+            if engine == "vector":
+                nc.vector.tensor_tensor(places, before, update[k][:], ALU.add)
+            else:
+                total = keep.tile([P, hi - lo], F32, name=f"total{k}")
+                nc.gpsimd.tensor_tensor(total[:], before, update[k][:], ALU.add)
+                nc.scalar.activation(places, total[:], ACT.Copy)
+
+        def fetch(k, engine, tag):
+            lo, hi = PIECES[k][:2]
+            old[k] = keep.tile([P, hi - lo], F32, name=f"old{k}", tag=tag, align_bytes=64)
+            columns = source[:].indirect(offsets[:, lo // 16 : hi // 16])
+            if engine == "vector":
+                nc.vector.tensor_copy(old[k][:], columns)
+            else:
+                nc.scalar.activation(old[k][:], columns, ACT.Copy)
+
+        last = len(PIECES) - 1
+        for k, (lo, hi, engine) in enumerate(PIECES):
+            gated(k, lo)
+            if k > 0:
+                weigh(k - 1)
+                put(k - 1)
+            for first in range(lo + CHUNK, hi, CHUNK):
+                gated(k, first)
+            g, c = divmod(hi // CHUNK - 1, CHUNKS)
+            if FETCH[k] == "vector":
+                fetch(k, "vector", f"act{g}{c}")
+            else:
+                fetch(k, "scalar", f"w_codes{k - 1}")
+            down(k)
+        weigh(last)
+        put(last)
         nc.sync.dma_start(out, window[:])

@@ -31,9 +31,8 @@ W_PIECES = (
         (256, 512, ((256, 512, "vector"),)),
     ),
 )
-PIECES = ((0, 256, "scalar"), (256, 512, "scalar"), (512, 768, "scalar"), (768, 1024, "vector"))
+PIECES = ((0, 256, "scalar"), (256, 512, "scalar"), (512, 768, "vector"), (768, 1024, "vector"))
 LOOSE_RUNS = (((0, HALF),), ((0, HALF // 2), (HALF // 2, HALF)))
-FETCH = ("vector", "scalar", "vector", "vector")
 SHARED = 256
 UP_BANKS = 3
 
@@ -56,6 +55,13 @@ def tile_picked_modres_glusilu_l_kernel(tc, xT, gate, res, w1, w3, w2_words, w2_
 
         nc.gpsimd.memset(w2_plane[:].bitcast(I32), 0)
 
+        nc.gpsimd.dma_start(w2_codes[:].bitcast(I32), w2_words[0].bitcast(I32))
+        for quadrant in range(4):
+            nc.gpsimd.dma_start(
+                w2_plane[32 * quadrant : 32 * quadrant + 4, :].bitcast(I32),
+                w2_scales[0, 4 * quadrant : 4 * quadrant + 4, :].bitcast(I32),
+            )
+
         raw = {}
         for u in range(2):
             for q, (lo, hi) in enumerate(X_PIECES[u]):
@@ -69,12 +75,6 @@ def tile_picked_modres_glusilu_l_kernel(tc, xT, gate, res, w1, w3, w2_words, w2_
             for q, (lo, hi, shares) in enumerate(W_PIECES[i]):
                 w_raw[i, q] = keep.tile([P, PACK, hi - lo], F32, name=f"w_raw{i}{q}")
                 nc.sync.dma_start(w_raw[i, q][:], w_rows[:, :, lo:hi])
-        nc.sync.dma_start(w2_codes[:].bitcast(I32), w2_words[0].bitcast(I32))
-        for quadrant in range(4):
-            nc.sync.dma_start(
-                w2_plane[32 * quadrant : 32 * quadrant + 4, :].bitcast(I32),
-                w2_scales[0, 4 * quadrant : 4 * quadrant + 4, :].bitcast(I32),
-            )
         source = keep.tile([P, T], F32, name="source")
         nc.sync.dma_start(source[:], res)
         gates = keep.tile([P, S], F32, name="gates")
@@ -115,7 +115,7 @@ def tile_picked_modres_glusilu_l_kernel(tc, xT, gate, res, w1, w3, w2_words, w2_
             x_codes.append(codes)
             x_plane.append(plane)
 
-        first_codes = keep.tile([P, HALF], U32, name="x_codes0", align_bytes=64)
+        first_codes = keep.tile([P, HALF], U32, name="x_codes0", tag="x_codes0", align_bytes=64)
         quantize_picked(0, first_codes[:])
 
         both = keep.tile([P, 2 * PACK * H - SHARED], BF16, name="w_grouped", tag="w_grouped", align_bytes=64)
@@ -161,25 +161,18 @@ def tile_picked_modres_glusilu_l_kernel(tc, xT, gate, res, w1, w3, w2_words, w2_
                 )
             return acc[:].rearrange("p t n -> p n t")
 
-        old = {}
-        act = {}
-
-        def silu(g, c):
-            act[g, c] = keep.tile([P, CHUNK, PACK], F32, name=f"act{g}{c}", tag=f"act{g}{c}", align_bytes=64)
-            nc.scalar.activation(act[g, c][:], up(0, g, c), ACT.Silu)
-
-        for c in range(CHUNKS):
-            silu(0, c)
         hidden = [keep.tile([P, hi - lo, PACK], BF16, name=f"hidden{lo}", align_bytes=64) for lo, hi, engine in PIECES]
+        act, y = {}, {}
+        update = keep.tile([P, S], F32, name="update")
 
-        def gated(k, first):
-            lo, hi, engine = PIECES[k]
-            g, c = divmod(first // CHUNK, CHUNKS)
-            nc.vector.tensor_tensor(hidden[k][:, first - lo : first - lo + CHUNK, :], up(1, g, c), act[g, c][:], ALU.mult)
-            if g == 0:
-                silu(1, c)
+        def silu(n):
+            act[n] = keep.tile([P, CHUNK, PACK], F32, name=f"act{n}", tag=f"act{n}")
+            nc.scalar.activation(act[n][:], up(0, *divmod(n, CHUNKS)), ACT.Silu)
 
-        y = {}
+        def gated(n):
+            k, c = divmod(n, 2)
+            dst = hidden[k][:, c * CHUNK : (c + 1) * CHUNK, :]
+            nc.vector.tensor_tensor(dst, up(1, *divmod(n, CHUNKS)), act[n][:], ALU.mult)
 
         def down(k):
             lo, hi, engine = PIECES[k]
@@ -189,59 +182,61 @@ def tile_picked_modres_glusilu_l_kernel(tc, xT, gate, res, w1, w3, w2_words, w2_
                 out=codes[:].bitcast(FP8X4), scales=plane[:], in_=hidden[k][:].rearrange("p n t -> p (n t)")
             )
             y[k] = psum_down.tile([P, hi - lo], F32, name="y")
-            for first in range(0, hi - lo, 256):
-                cols = slice(first, min(first + 256, hi - lo))
-                nc.tensor.matmul_mx(
-                    out=y[k][:, cols],
-                    lhsT=w2_codes[:].bitcast(FP4X4),
-                    lhsT_scale=w2_plane[:],
-                    rhs=codes[:, cols].bitcast(FP8X4),
-                    rhs_scale=plane[:, cols],
-                    start=True,
-                    stop=True,
-                )
-
-        update = {}
+            nc.tensor.matmul_mx(
+                out=y[k][:],
+                lhsT=w2_codes[:].bitcast(FP4X4),
+                lhsT_scale=w2_plane[:],
+                rhs=codes[:].bitcast(FP8X4),
+                rhs_scale=plane[:],
+                start=True,
+                stop=True,
+            )
 
         def weigh(k):
             lo, hi, engine = PIECES[k]
-            update[k] = keep.tile([P, hi - lo], F32, name=f"update{k}")
-            nc.vector.tensor_tensor(update[k][:], y[k][:], gates[:, lo:hi], ALU.mult)
+            nc.vector.tensor_tensor(update[:, lo:hi], y[k][:], gates[:, lo:hi], ALU.mult)
 
-        def put(k):
+        def fetch(k):
+            lo, hi, engine = PIECES[k]
+            nc.scalar.activation(old[:, lo:hi], source[:].indirect(offsets[:, lo // 16 : hi // 16]), ACT.Copy)
+
+        def put(k, before):
             lo, hi, engine = PIECES[k]
             places = window[:].indirect(offsets[:, lo // 16 : hi // 16])
-            before = old[k][:]
             if engine == "vector":
-                nc.vector.tensor_tensor(places, before, update[k][:], ALU.add)
+                nc.vector.tensor_tensor(places, before, update[:, lo:hi], ALU.add)
             else:
                 total = keep.tile([P, hi - lo], F32, name=f"total{k}")
-                nc.gpsimd.tensor_tensor(total[:], before, update[k][:], ALU.add)
+                nc.gpsimd.tensor_tensor(total[:], before, update[:, lo:hi], ALU.add)
                 nc.scalar.activation(places, total[:], ACT.Copy)
 
-        def fetch(k, engine, tag):
-            lo, hi = PIECES[k][:2]
-            old[k] = keep.tile([P, hi - lo], F32, name=f"old{k}", tag=tag, align_bytes=64)
-            columns = source[:].indirect(offsets[:, lo // 16 : hi // 16])
-            if engine == "vector":
-                nc.vector.tensor_copy(old[k][:], columns)
-            else:
-                nc.scalar.activation(old[k][:], columns, ACT.Copy)
-
-        last = len(PIECES) - 1
-        for k, (lo, hi, engine) in enumerate(PIECES):
-            gated(k, lo)
-            if k > 0:
-                weigh(k - 1)
-                put(k - 1)
-            for first in range(lo + CHUNK, hi, CHUNK):
-                gated(k, first)
-            g, c = divmod(hi // CHUNK - 1, CHUNKS)
-            if FETCH[k] == "vector":
-                fetch(k, "vector", f"act{g}{c}")
-            else:
-                fetch(k, "scalar", f"w_codes{k - 1}")
-            down(k)
-        weigh(last)
-        put(last)
+        for n in range(5):
+            silu(n)
+        for n in range(3):
+            gated(n)
+        silu(5)
+        down(0)
+        gated(3)
+        old = keep.tile([P, HALF], F32, name="old", tag="x_codes0", align_bytes=64)
+        fetch(0)
+        silu(6)
+        fetch(1)
+        silu(7)
+        gated(4)
+        weigh(0)
+        put(0, old[:, 0:256])
+        down(1)
+        gated(5)
+        gated(6)
+        weigh(1)
+        put(1, old[:, 256:512])
+        down(2)
+        gated(7)
+        late = keep.tile([P, HALF], F32, name="late", tag="act7")
+        nc.vector.tensor_copy(late[:], source[:].indirect(entries(1)))
+        weigh(2)
+        down(3)
+        put(2, late[:, 0:256])
+        weigh(3)
+        put(3, late[:, 256:512])
         nc.sync.dma_start(out, window[:])

@@ -115,7 +115,7 @@ def tile_picked_modres_glusilu_l_kernel(tc, xT, gate, res, w1, w3, w2_words, w2_
             x_codes.append(codes)
             x_plane.append(plane)
 
-        first_codes = keep.tile([P, HALF], U32, name="x_codes0", tag="x_codes0", align_bytes=64)
+        first_codes = keep.tile([P, HALF], U32, name="x_codes0", align_bytes=64)
         quantize_picked(0, first_codes[:])
 
         both = keep.tile([P, 2 * PACK * H - SHARED], BF16, name="w_grouped", tag="w_grouped", align_bytes=64)
@@ -196,9 +196,10 @@ def tile_picked_modres_glusilu_l_kernel(tc, xT, gate, res, w1, w3, w2_words, w2_
             lo, hi, engine = PIECES[k]
             nc.vector.tensor_tensor(update[:, lo:hi], y[k][:], gates[:, lo:hi], ALU.mult)
 
-        def fetch(k):
-            lo, hi, engine = PIECES[k]
-            nc.scalar.activation(old[:, lo:hi], source[:].indirect(offsets[:, lo // 16 : hi // 16]), ACT.Copy)
+        def fetch(lo, hi, n):
+            old = keep.tile([P, hi - lo], F32, name=f"old{lo}", tag=f"act{n}")
+            nc.vector.tensor_copy(old[:], source[:].indirect(offsets[:, lo // 16 : hi // 16]))
+            return old
 
         def put(k, before):
             lo, hi, engine = PIECES[k]
@@ -217,25 +218,23 @@ def tile_picked_modres_glusilu_l_kernel(tc, xT, gate, res, w1, w3, w2_words, w2_
         silu(5)
         down(0)
         gated(3)
-        old = keep.tile([P, HALF], F32, name="old", tag="x_codes0", align_bytes=64)
-        fetch(0)
         silu(6)
-        fetch(1)
         silu(7)
-        gated(4)
+        first = fetch(0, 256, 3)
         weigh(0)
-        put(0, old[:, 0:256])
         down(1)
+        put(0, first[:])
+        gated(4)
         gated(5)
-        gated(6)
+        second = fetch(256, 512, 5)
         weigh(1)
-        put(1, old[:, 256:512])
         down(2)
+        put(1, second[:])
+        gated(6)
         gated(7)
-        late = keep.tile([P, HALF], F32, name="late", tag="act7")
-        nc.vector.tensor_copy(late[:], source[:].indirect(entries(1)))
         weigh(2)
         down(3)
+        late = fetch(512, 1024, 7)
         put(2, late[:, 0:256])
         weigh(3)
         put(3, late[:, 256:512])

@@ -31,7 +31,7 @@ W_PIECES = (
         (256, 512, ((256, 512, "vector"),)),
     ),
 )
-PIECES = ((0, 256, "scalar"), (256, 512, "scalar"), (512, 768, "vector"), (768, 1024, "vector"))
+PIECES = ((0, 256, "scalar"), (256, 512, "scalar"), (512, 1024, "vector"))
 LOOSE_RUNS = (((0, HALF),), ((0, HALF // 2), (HALF // 2, HALF)))
 SHARED = 256
 UP_BANKS = 3
@@ -170,8 +170,9 @@ def tile_picked_modres_glusilu_l_kernel(tc, xT, gate, res, w1, w3, w2_words, w2_
             nc.scalar.activation(act[n][:], up(0, *divmod(n, CHUNKS)), ACT.Silu)
 
         def gated(n):
-            k, c = divmod(n, 2)
-            dst = hidden[k][:, c * CHUNK : (c + 1) * CHUNK, :]
+            k = min(n // 2, len(PIECES) - 1)
+            first = n * CHUNK - PIECES[k][0]
+            dst = hidden[k][:, first : first + CHUNK, :]
             nc.vector.tensor_tensor(dst, up(1, *divmod(n, CHUNKS)), act[n][:], ALU.mult)
 
         def down(k):
@@ -223,19 +224,17 @@ def tile_picked_modres_glusilu_l_kernel(tc, xT, gate, res, w1, w3, w2_words, w2_
         first = fetch(0, 256, 3)
         weigh(0)
         down(1)
+        second = keep.tile([P, 256], F32, name="second", tag="w_codes0", align_bytes=64)
+        nc.scalar.activation(second[:], source[:].indirect(offsets[:, 256 // 16 : 512 // 16]), ACT.Copy)
         put(0, first[:])
         gated(4)
         gated(5)
-        second = fetch(256, 512, 5)
         weigh(1)
-        down(2)
         put(1, second[:])
         gated(6)
         gated(7)
-        weigh(2)
-        down(3)
+        down(2)
         late = fetch(512, 1024, 7)
-        put(2, late[:, 0:256])
-        weigh(3)
-        put(3, late[:, 256:512])
+        weigh(2)
+        put(2, late[:])
         nc.sync.dma_start(out, window[:])

@@ -28,7 +28,7 @@ W_PIECES = (
     ((0, 256, ((0, 256, "scalar"),)), (256, 512, ((256, 336, "gpsimd"), (336, 512, "scalar")))),
     (
         (0, 256, ((0, 256, "scalar"),)),
-        (256, 512, ((256, 512, "vector"),)),
+        (256, 512, ((256, 352, "scalar"), (352, 512, "vector"))),
     ),
 )
 PIECES = ((0, 256, "scalar"), (256, 512, "scalar"), (512, 1024, "vector"))
@@ -161,44 +161,49 @@ def tile_picked_modres_glusilu_l_kernel(tc, xT, gate, res, w1, w3, w2_words, w2_
                 )
             return acc[:].rearrange("p t n -> p n t")
 
-        hidden = [keep.tile([P, hi - lo, PACK], BF16, name=f"hidden{lo}", align_bytes=64) for lo, hi, engine in PIECES]
+        hidden = [
+            keep.tile([P, 2 * CHUNK, PACK], BF16, name=f"hidden{r}", tag=f"hidden{r}", align_bytes=64)
+            for r in range(S // (2 * CHUNK))
+        ]
         act, y = {}, {}
         update = keep.tile([P, S], F32, name="update")
 
         def silu(n):
-            act[n] = keep.tile([P, CHUNK, PACK], F32, name=f"act{n}", tag=f"act{n}")
+            act[n] = keep.tile([P, CHUNK, PACK], F32, name=f"act{n}", tag=f"act{n}", align_bytes=64)
             nc.scalar.activation(act[n][:], up(0, *divmod(n, CHUNKS)), ACT.Silu)
 
         def gated(n):
-            k = min(n // 2, len(PIECES) - 1)
-            first = n * CHUNK - PIECES[k][0]
-            dst = hidden[k][:, first : first + CHUNK, :]
+            dst = hidden[n // 2][:, n % 2 * CHUNK : (n % 2 + 1) * CHUNK, :]
             nc.vector.tensor_tensor(dst, up(1, *divmod(n, CHUNKS)), act[n][:], ALU.mult)
 
-        def down(k):
+        def down(k, tag):
             lo, hi, engine = PIECES[k]
-            codes = keep.tile([P, hi - lo], U32, name=f"h_codes{k}", align_bytes=64)
+            codes = keep.tile([P, hi - lo], U32, name=f"h_codes{k}", tag=tag, align_bytes=64)
             plane = keep.tile([P, hi - lo], U8, name=f"h_plane{k}", align_bytes=64)
-            nc.vector.quantize_mx(
-                out=codes[:].bitcast(FP8X4), scales=plane[:], in_=hidden[k][:].rearrange("p n t -> p (n t)")
-            )
             y[k] = psum_down.tile([P, hi - lo], F32, name="y")
-            nc.tensor.matmul_mx(
-                out=y[k][:],
-                lhsT=w2_codes[:].bitcast(FP4X4),
-                lhsT_scale=w2_plane[:],
-                rhs=codes[:].bitcast(FP8X4),
-                rhs_scale=plane[:],
-                start=True,
-                stop=True,
-            )
+            for first in range(0, hi - lo, 2 * CHUNK):
+                cols = slice(first, first + 2 * CHUNK)
+                nc.vector.quantize_mx(
+                    out=codes[:, cols].bitcast(FP8X4),
+                    scales=plane[:, cols],
+                    in_=hidden[(lo + first) // (2 * CHUNK)][:].rearrange("p n t -> p (n t)"),
+                )
+                nc.tensor.matmul_mx(
+                    out=y[k][:, cols],
+                    lhsT=w2_codes[:].bitcast(FP4X4),
+                    lhsT_scale=w2_plane[:],
+                    rhs=codes[:, cols].bitcast(FP8X4),
+                    rhs_scale=plane[:, cols],
+                    start=True,
+                    stop=True,
+                )
 
         def weigh(k):
             lo, hi, engine = PIECES[k]
             nc.vector.tensor_tensor(update[:, lo:hi], y[k][:], gates[:, lo:hi], ALU.mult)
 
-        def fetch(lo, hi, n):
-            old = keep.tile([P, hi - lo], F32, name=f"old{lo}", tag=f"act{n}")
+        def fetch(lo, hi, tag):
+            old = keep.tile([P, hi - lo], F32, name=f"old{lo}", tag=tag, align_bytes=64)
             nc.vector.tensor_copy(old[:], source[:].indirect(offsets[:, lo // 16 : hi // 16]))
             return old
 
@@ -217,24 +222,24 @@ def tile_picked_modres_glusilu_l_kernel(tc, xT, gate, res, w1, w3, w2_words, w2_
         for n in range(3):
             gated(n)
         silu(5)
-        down(0)
+        down(0, "h_codes0")
         gated(3)
         silu(6)
         silu(7)
-        first = fetch(0, 256, 3)
+        first = fetch(0, 256, "act2")
+        down(1, "h_codes1")
         weigh(0)
-        down(1)
         second = keep.tile([P, 256], F32, name="second", tag="w_codes0", align_bytes=64)
         nc.scalar.activation(second[:], source[:].indirect(offsets[:, 256 // 16 : 512 // 16]), ACT.Copy)
         put(0, first[:])
         gated(4)
-        gated(5)
         weigh(1)
         put(1, second[:])
+        gated(5)
         gated(6)
         gated(7)
-        down(2)
-        late = fetch(512, 1024, 7)
+        down(2, "act6")
+        late = fetch(512, 1024, "hidden2")
         weigh(2)
         put(2, late[:])
         nc.sync.dma_start(out, window[:])

@@ -25,7 +25,7 @@ CHUNKS = HALF // CHUNK
 X_PIECES = (((0, 1024), (1024, 1536), (1536, 2048)), ((0, 1024), (1024, 1536), (1536, 1792), (1792, 2048)))
 X_SCALAR = ((0, 0, 176), (1024, 0, 0, 96))
 W_PIECES = (
-    ((0, 256, ((0, 256, "scalar"),)), (256, 512, ((256, 336, "gpsimd"), (336, 512, "scalar")))),
+    ((0, 256, ((0, 256, "scalar"),)), (256, 512, ((256, 512, "scalar"),))),
     (
         (0, 256, ((0, 256, "scalar"),)),
         (256, 512, ((256, 352, "scalar"), (352, 512, "vector"))),
@@ -73,7 +73,7 @@ def tile_picked_modres_glusilu_l_kernel(tc, xT, gate, res, w1, w3, w2_words, w2_
         for i, w in enumerate((w1, w3)):
             w_rows = w.rearrange("(p j) c -> p j c", j=PACK)
             for q, (lo, hi, shares) in enumerate(W_PIECES[i]):
-                w_raw[i, q] = keep.tile([P, PACK, hi - lo], F32, name=f"w_raw{i}{q}")
+                w_raw[i, q] = keep.tile([P, PACK, hi - lo], F32, name=f"w_raw{i}{q}", tag=f"w_raw{i}{q}", align_bytes=64)
                 nc.sync.dma_start(w_raw[i, q][:], w_rows[:, :, lo:hi])
         source = keep.tile([P, T], F32, name="source")
         nc.sync.dma_start(source[:], res)
@@ -128,8 +128,6 @@ def tile_picked_modres_glusilu_l_kernel(tc, xT, gate, res, w1, w3, w2_words, w2_
                     src = w_raw[i, q][:, :, lo - first : hi - first].rearrange("p j (m t) -> p m t j", t=PACK)
                     if engine == "vector":
                         nc.vector.tensor_copy(dst, src)
-                    elif engine == "gpsimd":
-                        nc.gpsimd.tensor_scalar(dst, src, 1.0, 0.0, ALU.mult, ALU.add)
                     else:
                         nc.scalar.copy(dst, src)
             codes = keep.tile([P, H], U32, name=f"w_codes{i}", tag=f"w_codes{i}", align_bytes=64)
@@ -166,15 +164,19 @@ def tile_picked_modres_glusilu_l_kernel(tc, xT, gate, res, w1, w3, w2_words, w2_
             for r in range(S // (2 * CHUNK))
         ]
         act, y = {}, {}
+        first_acts = keep.tile([P, UP_BANKS, CHUNK, PACK], F32, name="first_acts", tag="w_raw11", align_bytes=64)
         update = keep.tile([P, S], F32, name="update")
 
         def silu(n):
-            act[n] = keep.tile([P, CHUNK, PACK], F32, name=f"act{n}", tag=f"act{n}", align_bytes=64)
-            nc.scalar.activation(act[n][:], up(0, *divmod(n, CHUNKS)), ACT.Silu)
+            if n < UP_BANKS:
+                act[n] = first_acts[:, n, :, :]
+            else:
+                act[n] = keep.tile([P, CHUNK, PACK], F32, name=f"act{n}", tag=f"act{n}", align_bytes=64)[:]
+            nc.scalar.activation(act[n], up(0, *divmod(n, CHUNKS)), ACT.Silu)
 
         def gated(n):
             dst = hidden[n // 2][:, n % 2 * CHUNK : (n % 2 + 1) * CHUNK, :]
-            nc.vector.tensor_tensor(dst, up(1, *divmod(n, CHUNKS)), act[n][:], ALU.mult)
+            nc.vector.tensor_tensor(dst, up(1, *divmod(n, CHUNKS)), act[n], ALU.mult)
 
         def down(k, tag):
             lo, hi, engine = PIECES[k]
@@ -226,7 +228,7 @@ def tile_picked_modres_glusilu_l_kernel(tc, xT, gate, res, w1, w3, w2_words, w2_
         gated(3)
         silu(6)
         silu(7)
-        first = fetch(0, 256, "act2")
+        first = fetch(0, 256, "w_raw11")
         down(1, "h_codes1")
         weigh(0)
         second = keep.tile([P, 256], F32, name="second", tag="w_codes0", align_bytes=64)

@@ -35,13 +35,14 @@ PIECES = ((0, 256, "scalar"), (256, 512, "scalar"), (512, 1024, "vector"))
 LOOSE_RUNS = (((0, HALF),), ((0, HALF // 2), (HALF // 2, HALF)))
 SHARED = 256
 UP_BANKS = 3
+LATER_BANKS = (1, 0, 2)
 
 
 def tile_picked_modres_glusilu_l_kernel(tc, xT, gate, res, w1, w3, w2_words, w2_scales, offs, out):
     nc = tc.nc
     with ExitStack() as ctx:
         keep = ctx.enter_context(tc.tile_pool(name="keep", bufs=1))
-        psum_up = ctx.enter_context(tc.psum_pool(name="psum_up", bufs=UP_BANKS))
+        psum_up = ctx.enter_context(tc.psum_pool(name="psum_up", bufs=1))
         psum_down = ctx.enter_context(tc.psum_pool(name="psum_down", bufs=2))
 
         offsets = keep.tile([P, S // 16], U16, name="offsets")
@@ -145,7 +146,12 @@ def tile_picked_modres_glusilu_l_kernel(tc, xT, gate, res, w1, w3, w2_words, w2_
         quantize_picked(1, second_codes[:])
 
         def up(i, g, c):
-            acc = psum_up.tile([P, PACK, CHUNK], F32, name=f"up{i}")
+            n = g * CHUNKS + c
+            if i == 0 and n >= UP_BANKS:
+                bank = LATER_BANKS[n % UP_BANKS]
+            else:
+                bank = n % UP_BANKS
+            acc = psum_up.tile([P, PACK, CHUNK], F32, name=f"up{i}{bank}", tag=f"up{i}{bank}")
             cols = slice(c * CHUNK, (c + 1) * CHUNK)
             for t in range(PACK):
                 nc.tensor.matmul_mx(

@@ -130,7 +130,7 @@ def tile_picked_modres_glusilu_l_kernel(tc, xT, gate, res, w1, w3, w2_words, w2_
                     if engine == "vector":
                         nc.vector.tensor_copy(dst, src)
                     else:
-                        nc.scalar.copy(dst, src)
+                        nc.scalar.copy(dst.rearrange("p m t j -> p m j t"), src.rearrange("p m t j -> p m j t"))
             codes = keep.tile([P, H], U32, name=f"w_codes{i}", tag=f"w_codes{i}", align_bytes=64)
             plane = keep.tile([P, H], U8, name=f"w_plane{i}", align_bytes=64)
             for side in range(2):

@@ -22,13 +22,14 @@ HALF = S // 2
 CHUNK = 128
 CHUNKS = HALF // CHUNK
 
-X_PIECES = (((0, 1024), (1024, 1536), (1536, 2048)), ((0, 1024), (1024, 1536), (1536, 1792), (1792, 2048)))
-X_SCALAR = ((0, 0, 176), (1024, 0, 0, 96))
+X_PIECES = (((0, 1280), (1280, 2048)), ((0, 1024), (1024, 1536), (1536, 1792), (1792, 2048)))
+X_SCALAR = ((384, 256), (1024, 0, 0, 96))
 W_PIECES = (
     ((0, 256, ((0, 256, "scalar"),)), (256, 512, ((256, 512, "scalar"),))),
     (
         (0, 256, ((0, 256, "scalar"),)),
-        (256, 512, ((256, 352, "scalar"), (352, 512, "vector"))),
+        (256, 384, ((256, 384, "vector"),)),
+        (384, 512, ((384, 512, "vector"),)),
     ),
 )
 PIECES = ((0, 256, "scalar"), (256, 512, "scalar"), (512, 1024, "vector"))
@@ -170,7 +171,7 @@ def tile_picked_modres_glusilu_l_kernel(tc, xT, gate, res, w1, w3, w2_words, w2_
             for r in range(S // (2 * CHUNK))
         ]
         act, y = {}, {}
-        first_acts = keep.tile([P, UP_BANKS, CHUNK, PACK], F32, name="first_acts", tag="w_raw11", align_bytes=64)
+        first_acts = keep.tile([P, UP_BANKS, CHUNK, PACK], F32, name="first_acts", tag="w_raw10", align_bytes=64)
         update = keep.tile([P, S], F32, name="update")
 
         def silu(n):
@@ -225,16 +226,16 @@ def tile_picked_modres_glusilu_l_kernel(tc, xT, gate, res, w1, w3, w2_words, w2_
                 nc.gpsimd.tensor_tensor(total[:], before, update[:, lo:hi], ALU.add)
                 nc.scalar.activation(places, total[:], ACT.Copy)
 
-        for n in range(5):
+        for n in range(UP_BANKS):
             silu(n)
-        for n in range(3):
+        for n in range(UP_BANKS):
             gated(n)
-        silu(5)
+            silu(UP_BANKS + n)
         down(0, "h_codes0")
         gated(3)
         silu(6)
         silu(7)
-        first = fetch(0, 256, "w_raw11")
+        first = fetch(0, 256, "w_raw10")
         down(1, "h_codes1")
         weigh(0)
         second = keep.tile([P, 256], F32, name="second", tag="w_codes0", align_bytes=64)

@@ -32,6 +32,7 @@ W_PIECES = (
         (384, 512, ((384, 512, "vector"),)),
     ),
 )
+SCALAR_GATHER = (256, 640)
 PIECES = ((0, 256, "scalar"), (256, 512, "scalar"), (512, 1024, "vector"))
 LOOSE_RUNS = (((0, HALF),), ((0, HALF // 2), (HALF // 2, HALF)))
 SHARED = 256
@@ -238,17 +239,18 @@ def tile_picked_modres_glusilu_l_kernel(tc, xT, gate, res, w1, w3, w2_words, w2_
         first = fetch(0, 256, "w_raw10")
         down(1, "h_codes1")
         weigh(0)
-        second = keep.tile([P, 256], F32, name="second", tag="w_codes0", align_bytes=64)
-        nc.scalar.activation(second[:], source[:].indirect(offsets[:, 256 // 16 : 512 // 16]), ACT.Copy)
+        lo, hi = SCALAR_GATHER
+        rest = keep.tile([P, S - lo], F32, name="rest", tag="w_codes0", align_bytes=64)
+        nc.scalar.activation(rest[:, : hi - lo], source[:].indirect(offsets[:, lo // 16 : hi // 16]), ACT.Copy)
         put(0, first[:])
         gated(4)
         weigh(1)
-        put(1, second[:])
+        put(1, rest[:, : HALF - lo])
         gated(5)
         gated(6)
         gated(7)
         down(2, "act6")
-        late = fetch(512, 1024, "hidden2")
+        nc.vector.tensor_copy(rest[:, hi - lo :], source[:].indirect(offsets[:, hi // 16 :]))
         weigh(2)
-        put(2, late[:])
+        put(2, rest[:, HALF - lo :])
         nc.sync.dma_start(out, window[:])

@@ -20,15 +20,14 @@ P = 128
 PACK = 4
 HALF = S // 2
 CHUNK = 128
-CHUNKS = HALF // CHUNK
 
-X_PIECES = (((0, 1280), (1280, 2048)), ((0, 1024), (1024, 1536), (1536, 1792), (1792, 2048)))
-X_SCALAR = ((384, 256), (1024, 0, 0, 96))
+X_PIECES = (((0, 1280), (1280, 2048)), ((0, 896), (896, 1792), (1792, 2048)))
+X_SCALAR = ((384, 256), (896, 256, 80))
 W_PIECES = (
-    ((0, 256, ((0, 256, "scalar"),)), (256, 512, ((256, 512, "scalar"),))),
+    ((0, 128, ((0, 128, "scalar"),)), (128, 320, ((128, 320, "scalar"),)), (320, 512, ((320, 512, "scalar"),))),
     (
         (0, 256, ((0, 256, "scalar"),)),
-        (256, 384, ((256, 384, "vector"),)),
+        (256, 384, ((256, 320, "scalar"), (320, 384, "vector"))),
         (384, 512, ((384, 512, "vector"),)),
     ),
 )
@@ -106,20 +105,19 @@ def tile_picked_modres_glusilu_l_kernel(tc, xT, gate, res, w1, w3, w2_words, w2_
                     nc.gpsimd.tensor_copy(picked[0][:, lo:hi, :], loose[:, :, lo:hi].rearrange("p u n -> p n u"))
             nc.vector.tensor_copy(picked[1][:, :, u], pairs[:].indirect(entries(1)))
 
-        x_codes, x_plane = [], []
+        x_codes, x_plane = {}, {}
 
-        def quantize_picked(g, codes):
-            plane = keep.tile([P, HALF], U8, name=f"x_plane{g}", align_bytes=64)
+        def quantize_picked(lo, hi, tag):
+            x_codes[lo] = keep.tile([P, hi - lo], U32, name=f"x_codes{lo}", tag=tag, align_bytes=64)
+            x_plane[lo] = keep.tile([P, hi - lo], U8, name=f"x_plane{lo}", align_bytes=64)
+            g, first = divmod(lo, HALF)
             nc.vector.quantize_mx(
-                out=codes.bitcast(FP8X4),
-                scales=plane[:],
-                in_=picked[g][:].rearrange("p n u -> p (n u)").bitcast(BF16),
+                out=x_codes[lo][:].bitcast(FP8X4),
+                scales=x_plane[lo][:],
+                in_=picked[g][:, first : first + hi - lo, :].rearrange("p n u -> p (n u)").bitcast(BF16),
             )
-            x_codes.append(codes)
-            x_plane.append(plane)
 
-        first_codes = keep.tile([P, HALF], U32, name="x_codes0", align_bytes=64)
-        quantize_picked(0, first_codes[:])
+        quantize_picked(0, 256, "x_codes0")
 
         both = keep.tile([P, 2 * PACK * H - SHARED], BF16, name="w_grouped", tag="w_grouped", align_bytes=64)
         w_codes, w_plane = [], []
@@ -133,6 +131,8 @@ def tile_picked_modres_glusilu_l_kernel(tc, xT, gate, res, w1, w3, w2_words, w2_
                         nc.vector.tensor_copy(dst, src)
                     else:
                         nc.scalar.copy(dst.rearrange("p m t j -> p m j t"), src.rearrange("p m t j -> p m j t"))
+            if i == 1:
+                quantize_picked(256, HALF, "w_raw02")
             codes = keep.tile([P, H], U32, name=f"w_codes{i}", tag=f"w_codes{i}", align_bytes=64)
             plane = keep.tile([P, H], U8, name=f"w_plane{i}", align_bytes=64)
             for side in range(2):
@@ -144,17 +144,16 @@ def tile_picked_modres_glusilu_l_kernel(tc, xT, gate, res, w1, w3, w2_words, w2_
             w_codes.append(codes)
             w_plane.append(plane)
 
-        second_codes = keep.tile([P, HALF], U32, name="x_codes1", tag="w_grouped", align_bytes=64)
-        quantize_picked(1, second_codes[:])
+        quantize_picked(HALF, S, "w_grouped")
 
-        def up(i, g, c):
-            n = g * CHUNKS + c
+        def up(i, n):
+            g = max(lo for lo in x_codes if lo <= n * CHUNK)
             if i == 0 and n >= UP_BANKS:
                 bank = LATER_BANKS[n % UP_BANKS]
             else:
                 bank = n % UP_BANKS
             acc = psum_up.tile([P, PACK, CHUNK], F32, name=f"up{i}{bank}", tag=f"up{i}{bank}")
-            cols = slice(c * CHUNK, (c + 1) * CHUNK)
+            cols = slice(n * CHUNK - g, (n + 1) * CHUNK - g)
             for t in range(PACK):
                 nc.tensor.matmul_mx(
                     out=acc[:, t, :],
@@ -180,11 +179,11 @@ def tile_picked_modres_glusilu_l_kernel(tc, xT, gate, res, w1, w3, w2_words, w2_
                 act[n] = first_acts[:, n, :, :]
             else:
                 act[n] = keep.tile([P, CHUNK, PACK], F32, name=f"act{n}", tag=f"act{n}", align_bytes=64)[:]
-            nc.scalar.activation(act[n], up(0, *divmod(n, CHUNKS)), ACT.Silu)
+            nc.scalar.activation(act[n], up(0, n), ACT.Silu)
 
         def gated(n):
             dst = hidden[n // 2][:, n % 2 * CHUNK : (n % 2 + 1) * CHUNK, :]
-            nc.vector.tensor_tensor(dst, up(1, *divmod(n, CHUNKS)), act[n], ALU.mult)
+            nc.vector.tensor_tensor(dst, up(1, n), act[n], ALU.mult)
 
         def down(k, tag):
             lo, hi, engine = PIECES[k]

@@ -36,7 +36,7 @@ PIECES = ((0, 256, "scalar"), (256, 512, "scalar"), (512, 1024, "vector"))
 LOOSE_RUNS = (((0, HALF),), ((0, HALF // 2), (HALF // 2, HALF)))
 SHARED = 256
 UP_BANKS = 3
-LATER_BANKS = (1, 0, 2)
+BANKS = ((0, 1, 2, 0, 4, 5, 0, 4), (3, 1, 2, 3, 1, 2, 5, 3))
 
 
 def tile_picked_modres_glusilu_l_kernel(tc, xT, gate, res, w1, w3, w2_words, w2_scales, offs, out):
@@ -107,17 +107,17 @@ def tile_picked_modres_glusilu_l_kernel(tc, xT, gate, res, w1, w3, w2_words, w2_
 
         x_codes, x_plane = {}, {}
 
-        def quantize_picked(lo, hi, tag):
-            x_codes[lo] = keep.tile([P, hi - lo], U32, name=f"x_codes{lo}", tag=tag, align_bytes=64)
+        def quantize_picked(lo, hi, codes):
+            x_codes[lo] = codes
             x_plane[lo] = keep.tile([P, hi - lo], U8, name=f"x_plane{lo}", align_bytes=64)
             g, first = divmod(lo, HALF)
             nc.vector.quantize_mx(
-                out=x_codes[lo][:].bitcast(FP8X4),
+                out=codes.bitcast(FP8X4),
                 scales=x_plane[lo][:],
                 in_=picked[g][:, first : first + hi - lo, :].rearrange("p n u -> p (n u)").bitcast(BF16),
             )
 
-        quantize_picked(0, 256, "x_codes0")
+        quantize_picked(0, 256, keep.tile([P, 256], U32, name="x_codes0", align_bytes=64)[:])
 
         both = keep.tile([P, 2 * PACK * H - SHARED], BF16, name="w_grouped", tag="w_grouped", align_bytes=64)
         w_codes, w_plane = [], []
@@ -132,7 +132,7 @@ def tile_picked_modres_glusilu_l_kernel(tc, xT, gate, res, w1, w3, w2_words, w2_
                     else:
                         nc.scalar.copy(dst.rearrange("p m t j -> p m j t"), src.rearrange("p m t j -> p m j t"))
             if i == 1:
-                quantize_picked(256, HALF, "w_raw02")
+                quantize_picked(256, 384, keep.tile([P, CHUNK], U32, name="x_codes2", tag="w_raw02", align_bytes=64)[:])
             codes = keep.tile([P, H], U32, name=f"w_codes{i}", tag=f"w_codes{i}", align_bytes=64)
             plane = keep.tile([P, H], U8, name=f"w_plane{i}", align_bytes=64)
             for side in range(2):
@@ -144,15 +144,13 @@ def tile_picked_modres_glusilu_l_kernel(tc, xT, gate, res, w1, w3, w2_words, w2_
             w_codes.append(codes)
             w_plane.append(plane)
 
-        quantize_picked(HALF, S, "w_grouped")
+        later_codes = keep.tile([P, S - 384], U32, name="x_codes_later", tag="w_grouped", align_bytes=64)
+        quantize_picked(384, HALF, later_codes[:, : HALF - 384])
+        quantize_picked(HALF, S, later_codes[:, HALF - 384 :])
 
         def up(i, n):
             g = max(lo for lo in x_codes if lo <= n * CHUNK)
-            if i == 0 and n >= UP_BANKS:
-                bank = LATER_BANKS[n % UP_BANKS]
-            else:
-                bank = n % UP_BANKS
-            acc = psum_up.tile([P, PACK, CHUNK], F32, name=f"up{i}{bank}", tag=f"up{i}{bank}")
+            acc = psum_up.tile([P, PACK, CHUNK], F32, name=f"up{BANKS[i][n]}", tag=f"up{BANKS[i][n]}")
             cols = slice(n * CHUNK - g, (n + 1) * CHUNK - g)
             for t in range(PACK):
                 nc.tensor.matmul_mx(

@@ -31,7 +31,7 @@ W_PIECES = (
         (384, 512, ((384, 512, "vector"),)),
     ),
 )
-SCALAR_GATHER = (256, 640)
+SCALAR_GATHER = 512
 PIECES = ((0, 256, "scalar"), (256, 512, "scalar"), (512, 1024, "vector"))
 LOOSE_RUNS = (((0, HALF),), ((0, HALF // 2), (HALF // 2, HALF)))
 SHARED = 256
@@ -187,16 +187,16 @@ def tile_picked_modres_glusilu_l_kernel(tc, xT, gate, res, w1, w3, w2_words, w2_
             lo, hi, engine = PIECES[k]
             codes = keep.tile([P, hi - lo], U32, name=f"h_codes{k}", tag=tag, align_bytes=64)
             plane = keep.tile([P, hi - lo], U8, name=f"h_plane{k}", align_bytes=64)
-            y[k] = psum_down.tile([P, hi - lo], F32, name="y")
             for first in range(0, hi - lo, 2 * CHUNK):
                 cols = slice(first, first + 2 * CHUNK)
+                y[lo + first] = psum_down.tile([P, 2 * CHUNK], F32, name="y")
                 nc.vector.quantize_mx(
                     out=codes[:, cols].bitcast(FP8X4),
                     scales=plane[:, cols],
                     in_=hidden[(lo + first) // (2 * CHUNK)][:].rearrange("p n t -> p (n t)"),
                 )
                 nc.tensor.matmul_mx(
-                    out=y[k][:, cols],
+                    out=y[lo + first][:],
                     lhsT=w2_codes[:].bitcast(FP4X4),
                     lhsT_scale=w2_plane[:],
                     rhs=codes[:, cols].bitcast(FP8X4),
@@ -207,21 +207,18 @@ def tile_picked_modres_glusilu_l_kernel(tc, xT, gate, res, w1, w3, w2_words, w2_
 
         def weigh(k):
             lo, hi, engine = PIECES[k]
-            nc.vector.tensor_tensor(update[:, lo:hi], y[k][:], gates[:, lo:hi], ALU.mult)
+            for first in range(lo, hi, 2 * CHUNK):
+                cols = slice(first, first + 2 * CHUNK)
+                nc.vector.tensor_tensor(update[:, cols], y[first][:], gates[:, cols], ALU.mult)
 
-        def fetch(lo, hi, tag):
-            old = keep.tile([P, hi - lo], F32, name=f"old{lo}", tag=tag, align_bytes=64)
-            nc.vector.tensor_copy(old[:], source[:].indirect(offsets[:, lo // 16 : hi // 16]))
-            return old
-
-        def put(k, before):
+        def put(k, old):
             lo, hi, engine = PIECES[k]
             places = window[:].indirect(offsets[:, lo // 16 : hi // 16])
             if engine == "vector":
-                nc.vector.tensor_tensor(places, before, update[:, lo:hi], ALU.add)
+                nc.vector.tensor_tensor(places, old[:, lo:hi], update[:, lo:hi], ALU.add)
             else:
                 total = keep.tile([P, hi - lo], F32, name=f"total{k}")
-                nc.gpsimd.tensor_tensor(total[:], before, update[:, lo:hi], ALU.add)
+                nc.gpsimd.tensor_tensor(total[:], old[:, lo:hi], update[:, lo:hi], ALU.add)
                 nc.scalar.activation(places, total[:], ACT.Copy)
 
         for n in range(UP_BANKS):
@@ -229,25 +226,24 @@ def tile_picked_modres_glusilu_l_kernel(tc, xT, gate, res, w1, w3, w2_words, w2_
         for n in range(UP_BANKS):
             gated(n)
             silu(UP_BANKS + n)
+        old = keep.tile([P, S], F32, name="old", tag="w_raw02", align_bytes=64)
+        nc.scalar.activation(old[:, :SCALAR_GATHER], source[:].indirect(offsets[:, : SCALAR_GATHER // 16]), ACT.Copy)
         down(0, "h_codes0")
         gated(3)
         silu(6)
         silu(7)
-        first = fetch(0, 256, "w_raw10")
+        nc.vector.tensor_copy(old[:, HALF : HALF + CHUNK], source[:].indirect(offsets[:, HALF // 16 : (HALF + CHUNK) // 16]))
         down(1, "h_codes1")
         weigh(0)
-        lo, hi = SCALAR_GATHER
-        rest = keep.tile([P, S - lo], F32, name="rest", tag="w_codes0", align_bytes=64)
-        nc.scalar.activation(rest[:, : hi - lo], source[:].indirect(offsets[:, lo // 16 : hi // 16]), ACT.Copy)
-        put(0, first[:])
+        put(0, old)
         gated(4)
         weigh(1)
-        put(1, rest[:, : HALF - lo])
+        put(1, old)
         gated(5)
         gated(6)
         gated(7)
         down(2, "act6")
-        nc.vector.tensor_copy(rest[:, hi - lo :], source[:].indirect(offsets[:, hi // 16 :]))
+        nc.vector.tensor_copy(old[:, HALF + CHUNK :], source[:].indirect(offsets[:, (HALF + CHUNK) // 16 :]))
         weigh(2)
-        put(2, rest[:, HALF - lo :])
+        put(2, old)
         nc.sync.dma_start(out, window[:])

@@ -27,11 +27,11 @@ W_PIECES = (
     ((0, 128, ((0, 128, "scalar"),)), (128, 320, ((128, 320, "scalar"),)), (320, 512, ((320, 512, "scalar"),))),
     (
         (0, 256, ((0, 256, "scalar"),)),
-        (256, 384, ((256, 320, "scalar"), (320, 384, "vector"))),
+        (256, 384, ((256, 384, "vector"),)),
         (384, 512, ((384, 512, "vector"),)),
     ),
 )
-SCALAR_GATHER = 512
+SCALAR_GATHER = 608
 PIECES = ((0, 256, "scalar"), (256, 512, "scalar"), (512, 1024, "vector"))
 LOOSE_RUNS = (((0, HALF),), ((0, HALF // 2), (HALF // 2, HALF)))
 SHARED = 256
@@ -152,7 +152,7 @@ def tile_picked_modres_glusilu_l_kernel(tc, xT, gate, res, w1, w3, w2_words, w2_
             g = max(lo for lo in x_codes if lo <= n * CHUNK)
             acc = psum_up.tile([P, PACK, CHUNK], F32, name=f"up{BANKS[i][n]}", tag=f"up{BANKS[i][n]}")
             cols = slice(n * CHUNK - g, (n + 1) * CHUNK - g)
-            for t in range(PACK):
+            for t in range(PACK) if n == 0 else (2, 3, 0, 1):
                 nc.tensor.matmul_mx(
                     out=acc[:, t, :],
                     lhsT=w_codes[i][:, t * P : (t + 1) * P].bitcast(FP8X4),
@@ -211,14 +211,14 @@ def tile_picked_modres_glusilu_l_kernel(tc, xT, gate, res, w1, w3, w2_words, w2_
                 cols = slice(first, first + 2 * CHUNK)
                 nc.vector.tensor_tensor(update[:, cols], y[first][:], gates[:, cols], ALU.mult)
 
-        def put(k, old):
+        def put(k, old, adder):
             lo, hi, engine = PIECES[k]
             places = window[:].indirect(offsets[:, lo // 16 : hi // 16])
             if engine == "vector":
                 nc.vector.tensor_tensor(places, old[:, lo:hi], update[:, lo:hi], ALU.add)
             else:
                 total = keep.tile([P, hi - lo], F32, name=f"total{k}")
-                nc.gpsimd.tensor_tensor(total[:], old[:, lo:hi], update[:, lo:hi], ALU.add)
+                adder.tensor_tensor(total[:], old[:, lo:hi], update[:, lo:hi], ALU.add)
                 nc.scalar.activation(places, total[:], ACT.Copy)
 
         for n in range(UP_BANKS):
@@ -232,18 +232,17 @@ def tile_picked_modres_glusilu_l_kernel(tc, xT, gate, res, w1, w3, w2_words, w2_
         gated(3)
         silu(6)
         silu(7)
-        nc.vector.tensor_copy(old[:, HALF : HALF + CHUNK], source[:].indirect(offsets[:, HALF // 16 : (HALF + CHUNK) // 16]))
-        down(1, "h_codes1")
-        weigh(0)
-        put(0, old)
         gated(4)
-        weigh(1)
-        put(1, old)
+        weigh(0)
+        down(1, "h_codes1")
+        put(0, old, nc.vector)
         gated(5)
+        weigh(1)
+        put(1, old, nc.gpsimd)
         gated(6)
         gated(7)
         down(2, "act6")
-        nc.vector.tensor_copy(old[:, HALF + CHUNK :], source[:].indirect(offsets[:, (HALF + CHUNK) // 16 :]))
+        nc.vector.tensor_copy(old[:, SCALAR_GATHER:], source[:].indirect(offsets[:, SCALAR_GATHER // 16 :]))
         weigh(2)
-        put(2, old)
+        put(2, old, nc.vector)
         nc.sync.dma_start(out, window[:])

@@ -31,9 +31,13 @@ W_PIECES = (
         (384, 512, ((384, 512, "vector"),)),
     ),
 )
-SCALAR_GATHER = 608
+SCALAR_GATHER = 640
 PIECES = ((0, 256, "scalar"), (256, 512, "scalar"), (512, 1024, "vector"))
 LOOSE_RUNS = (((0, HALF),), ((0, HALF // 2), (HALF // 2, HALF)))
+W_CALLS = (
+    ((0, H // 2), (H // 2, H)),
+    tuple((P * t + half, P * t + half + P // 2) for half in (0, P // 2) for t in range(PACK)),
+)
 SHARED = 256
 UP_BANKS = 3
 BANKS = ((0, 1, 2, 0, 4, 5, 0, 4), (3, 1, 2, 3, 1, 2, 5, 3))
@@ -131,18 +135,18 @@ def tile_picked_modres_glusilu_l_kernel(tc, xT, gate, res, w1, w3, w2_words, w2_
                         nc.vector.tensor_copy(dst, src)
                     else:
                         nc.scalar.copy(dst.rearrange("p m t j -> p m j t"), src.rearrange("p m t j -> p m j t"))
-            if i == 1:
-                quantize_picked(256, 384, keep.tile([P, CHUNK], U32, name="x_codes2", tag="w_raw02", align_bytes=64)[:])
-            codes = keep.tile([P, H], U32, name=f"w_codes{i}", tag=f"w_codes{i}", align_bytes=64)
+            codes = keep.tile([P, H], U32, name=f"w_codes{i}", tag=("w_codes0", "w_raw11")[i], align_bytes=64)
             plane = keep.tile([P, H], U8, name=f"w_plane{i}", align_bytes=64)
-            for side in range(2):
+            for lo, hi in W_CALLS[i]:
                 nc.vector.quantize_mx(
-                    out=codes[:, side * (H // 2) : (side + 1) * (H // 2)].bitcast(FP8X4),
-                    scales=plane[:, side * (H // 2) : (side + 1) * (H // 2)],
-                    in_=grouped[:, side * 2 * H : (side + 1) * 2 * H],
+                    out=codes[:, lo:hi].bitcast(FP8X4),
+                    scales=plane[:, lo:hi],
+                    in_=grouped[:, PACK * lo : PACK * hi],
                 )
             w_codes.append(codes)
             w_plane.append(plane)
+            if i == 0:
+                quantize_picked(256, 384, keep.tile([P, CHUNK], U32, name="x_codes2", tag="w_raw02", align_bytes=64)[:])
 
         later_codes = keep.tile([P, S - 384], U32, name="x_codes_later", tag="w_grouped", align_bytes=64)
         quantize_picked(384, HALF, later_codes[:, : HALF - 384])
@@ -152,7 +156,7 @@ def tile_picked_modres_glusilu_l_kernel(tc, xT, gate, res, w1, w3, w2_words, w2_
             g = max(lo for lo in x_codes if lo <= n * CHUNK)
             acc = psum_up.tile([P, PACK, CHUNK], F32, name=f"up{BANKS[i][n]}", tag=f"up{BANKS[i][n]}")
             cols = slice(n * CHUNK - g, (n + 1) * CHUNK - g)
-            for t in range(PACK) if n == 0 else (2, 3, 0, 1):
+            for t in range(PACK) if n == 0 else (3, 0, 1, 2):
                 nc.tensor.matmul_mx(
                     out=acc[:, t, :],
                     lhsT=w_codes[i][:, t * P : (t + 1) * P].bitcast(FP8X4),

@@ -21,10 +21,10 @@ PACK = 4
 HALF = S // 2
 CHUNK = 128
 
-X_PIECES = (((0, 1280), (1280, 2048)), ((0, 896), (896, 1792), (1792, 2048)))
-X_SCALAR = ((384, 256), (896, 256, 80))
+X_PIECES = (((0, 1024), (1024, 2048)), ((0, 896), (896, 1792), (1792, 2048)))
+X_SCALAR = ((320, 320), (896, 256, 80))
 W_PIECES = (
-    ((0, 128, ((0, 128, "scalar"),)), (128, 320, ((128, 320, "scalar"),)), (320, 512, ((320, 512, "scalar"),))),
+    ((0, 128, ((0, 128, "scalar"),)), (128, 256, ((128, 256, "scalar"),)), (256, 512, ((256, 512, "scalar"),))),
     (
         (0, 256, ((0, 256, "scalar"),)),
         (256, 384, ((256, 384, "vector"),)),
@@ -34,11 +34,6 @@ W_PIECES = (
 SCALAR_GATHER = 640
 PIECES = ((0, 256, "scalar"), (256, 512, "scalar"), (512, 1024, "vector"))
 LOOSE_RUNS = (((0, HALF),), ((0, HALF // 2), (HALF // 2, HALF)))
-W_CALLS = (
-    ((0, H // 2), (H // 2, H)),
-    tuple((P * t + half, P * t + half + P // 2) for half in (0, P // 2) for t in range(PACK)),
-)
-SHARED = 256
 UP_BANKS = 3
 BANKS = ((0, 1, 2, 0, 4, 5, 0, 4), (3, 1, 2, 3, 1, 2, 5, 3))
 
@@ -123,13 +118,24 @@ def tile_picked_modres_glusilu_l_kernel(tc, xT, gate, res, w1, w3, w2_words, w2_
 
         quantize_picked(0, 256, keep.tile([P, 256], U32, name="x_codes0", align_bytes=64)[:])
 
-        both = keep.tile([P, 2 * PACK * H - SHARED], BF16, name="w_grouped", tag="w_grouped", align_bytes=64)
         w_codes, w_plane = [], []
         for i in range(2):
-            grouped = both[:, (1 - i) * (PACK * H - SHARED) : (1 - i) * (PACK * H - SHARED) + PACK * H]
+            if i == 0:
+                whole = keep.tile([P, PACK, P, PACK], BF16, name="w1_grouped", tag="w_grouped", align_bytes=64)
+                halves = [whole[:, :, : P // 2, :], whole[:, :, P // 2 :, :]]
+            else:
+                halves = [
+                    keep.tile([P, PACK, P // 2, PACK], BF16, name="w3_low", align_bytes=64)[:],
+                    keep.tile([P, PACK, P // 2, PACK], BF16, name="w3_high", tag="w_grouped", align_bytes=64)[:],
+                ]
             for q, (first, last, shares) in enumerate(W_PIECES[i]):
                 for lo, hi, engine in shares:
-                    dst = grouped.rearrange("p (t m j) -> p m t j", t=PACK, j=PACK)[:, lo // PACK : hi // PACK, :, :]
+                    if i == 0:
+                        dst = whole[:, :, lo // PACK : hi // PACK, :]
+                    else:
+                        half, start = divmod(lo, H // 2)
+                        dst = halves[half][:, :, start // PACK : (start + hi - lo) // PACK, :]
+                    dst = dst.rearrange("p t m j -> p m t j")
                     src = w_raw[i, q][:, :, lo - first : hi - first].rearrange("p j (m t) -> p m t j", t=PACK)
                     if engine == "vector":
                         nc.vector.tensor_copy(dst, src)
@@ -137,12 +143,13 @@ def tile_picked_modres_glusilu_l_kernel(tc, xT, gate, res, w1, w3, w2_words, w2_
                         nc.scalar.copy(dst.rearrange("p m t j -> p m j t"), src.rearrange("p m t j -> p m j t"))
             codes = keep.tile([P, H], U32, name=f"w_codes{i}", tag=("w_codes0", "w_raw11")[i], align_bytes=64)
             plane = keep.tile([P, H], U8, name=f"w_plane{i}", align_bytes=64)
-            for lo, hi in W_CALLS[i]:
-                nc.vector.quantize_mx(
-                    out=codes[:, lo:hi].bitcast(FP8X4),
-                    scales=plane[:, lo:hi],
-                    in_=grouped[:, PACK * lo : PACK * hi],
-                )
+            calls = [
+                (P * t + half * (P // 2), P // 2, halves[half][:, t].rearrange("p m j -> p (m j)"))
+                for half in range(2)
+                for t in range(PACK)
+            ]
+            for lo, width, values in calls:
+                nc.vector.quantize_mx(out=codes[:, lo : lo + width].bitcast(FP8X4), scales=plane[:, lo : lo + width], in_=values)
             w_codes.append(codes)
             w_plane.append(plane)
             if i == 0:

@@ -18,44 +18,40 @@ ACT = mybir.ActivationFunctionType
 
 P = 128
 PACK = 4
-HALF = S // 2
 CHUNK = 128
-
-X_PIECES = (((0, 1024), (1024, 2048)), ((0, 896), (896, 1792), (1792, 2048)))
-X_SCALAR = ((320, 320), (896, 256, 80))
+PIECE = 256
+X_VECTOR = 384
+X_LAST = 640
+LATE_SCALAR = 0
 W_PIECES = (
-    ((0, 128, ((0, 128, "scalar"),)), (128, 256, ((128, 256, "scalar"),)), (256, 512, ((256, 512, "scalar"),))),
-    (
-        (0, 256, ((0, 256, "scalar"),)),
-        (256, 384, ((256, 384, "vector"),)),
-        (384, 512, ((384, 512, "vector"),)),
-    ),
+    ((0, 256, "vector"), (256, 512, "scalar")),
+    ((0, 256, "scalar"), (256, 384, "vector"), (384, 512, "vector")),
 )
-SCALAR_GATHER = 640
-PIECES = ((0, 256, "scalar"), (256, 512, "scalar"), (512, 1024, "vector"))
-LOOSE_RUNS = (((0, HALF),), ((0, HALF // 2), (HALF // 2, HALF)))
-UP_BANKS = 3
-BANKS = ((0, 1, 2, 0, 4, 5, 0, 4), (3, 1, 2, 3, 1, 2, 5, 3))
+A_BANKS, B_BANKS = 3, 4
+BANKS = ((0, 1, 2, 0, 1, 2, 4, 6), (3, 4, 5, 6, 3, 0, 5, 3))
+ACT_PLACES = (7168, 4608, 2560)
 
 
 def tile_picked_modres_glusilu_l_kernel(tc, xT, gate, res, w1, w3, w2_words, w2_scales, offs, out):
     nc = tc.nc
     with ExitStack() as ctx:
         keep = ctx.enter_context(tc.tile_pool(name="keep", bufs=1))
-        psum_up = ctx.enter_context(tc.psum_pool(name="psum_up", bufs=1))
-        psum_down = ctx.enter_context(tc.psum_pool(name="psum_down", bufs=2))
+        placed = ctx.enter_context(tc.tile_pool(name="placed", bufs=1))
+        psum = ctx.enter_context(tc.psum_pool(name="psum", bufs=1))
 
         offsets = keep.tile([P, S // 16], U16, name="offsets")
         x_rows = xT.rearrange("(p j) n -> p j n", j=PACK)
         w2_codes = keep.tile([P, 2 * N], U8, name="w2_codes", align_bytes=64)
         w2_plane = keep.tile([P, N], U8, name="w2_plane", align_bytes=64)
 
+        def entries(lo, hi):
+            return offsets[:, lo // 16 : hi // 16]
+
         warm = keep.tile([P, 2], F32, name="warm")
         nc.gpsimd.memset(warm[:, 0:1], 0.0)
         nc.scalar.activation(warm[:, 1:2], warm[:, 0:1], ACT.Silu)
 
         nc.gpsimd.memset(w2_plane[:].bitcast(I32), 0)
-
         nc.gpsimd.dma_start(w2_codes[:].bitcast(I32), w2_words[0].bitcast(I32))
         for quadrant in range(4):
             nc.gpsimd.dma_start(
@@ -63,105 +59,87 @@ def tile_picked_modres_glusilu_l_kernel(tc, xT, gate, res, w1, w3, w2_words, w2_
                 w2_scales[0, 4 * quadrant : 4 * quadrant + 4, :].bitcast(I32),
             )
 
-        raw = {}
-        for u in range(2):
-            for q, (lo, hi) in enumerate(X_PIECES[u]):
-                raw[u, q] = keep.tile([P, 2, hi - lo], F32, name=f"x_raw{u}{q}")
-                nc.sync.dma_start(raw[u, q][:], x_rows[:, 2 * u : 2 * u + 2, lo:hi])
-                if (u, q) == (0, 0):
-                    nc.sync.dma_start(offsets[:], offs)
+        planes = []
+        for j in range(PACK):
+            planes.append(keep.tile([P, T], F32, name=f"x_raw{j}"))
+            nc.sync.dma_start(planes[j][:], x_rows[:, j, :])
+            if j == 0:
+                nc.sync.dma_start(offsets[:], offs)
         w_raw = {}
         for i, w in enumerate((w1, w3)):
             w_rows = w.rearrange("(p j) c -> p j c", j=PACK)
-            for q, (lo, hi, shares) in enumerate(W_PIECES[i]):
-                w_raw[i, q] = keep.tile([P, PACK, hi - lo], F32, name=f"w_raw{i}{q}", tag=f"w_raw{i}{q}", align_bytes=64)
+            for q, (lo, hi, engine) in enumerate(W_PIECES[i]):
+                if (i, q) == (1, 0):
+                    w_raw[i, q] = placed.tile([P, PACK, hi - lo], F32, name="w_raw10", offset=4096, align_bytes=64)
+                else:
+                    w_raw[i, q] = keep.tile([P, PACK, hi - lo], F32, name=f"w_raw{i}{q}", tag=f"w_raw{i}{q}", align_bytes=64)
                 nc.sync.dma_start(w_raw[i, q][:], w_rows[:, :, lo:hi])
         source = keep.tile([P, T], F32, name="source")
         nc.sync.dma_start(source[:], res)
-        gates = keep.tile([P, S], F32, name="gates")
-        nc.sync.dma_start(gates[:], gate)
+        gates = [keep.tile([P, S // 2], F32, name=f"gates{g}") for g in range(2)]
+        nc.sync.dma_start(gates[0][:], gate[:, : S // 2])
         window = keep.tile([P, T], F32, name="window")
         nc.sync.dma_start(window[:], res)
+        nc.sync.dma_start(gates[1][:], gate[:, S // 2 :])
 
-        def entries(g):
-            return offsets[:, g * (HALF // 16) : (g + 1) * (HALF // 16)]
-
-        picked = [keep.tile([P, HALF, 2], U32, name=f"picked{g}", align_bytes=64) for g in range(2)]
-        loose = keep.tile([P, 2, HALF], U32, name="loose")
-        for u in range(2):
-            pairs = keep.tile([P, T], U32, name=f"pairs{u}")
-            for q, (lo, hi) in enumerate(X_PIECES[u]):
-                dst = pairs[:, lo:hi].bitcast(BF16).rearrange("p (n j) -> p n j", j=2)
-                src = raw[u, q][:].rearrange("p j n -> p n j")
-                share = X_SCALAR[u][q]
-                if share > 0:
-                    nc.scalar.copy(dst[:, :share, :], src[:, :share, :])
-                if share < hi - lo:
-                    nc.vector.tensor_copy(dst[:, share:, :], src[:, share:, :])
-            for lo, hi in LOOSE_RUNS[u]:
-                nc.vector.tensor_copy(loose[:, u, lo:hi], pairs[:].indirect(offsets[:, lo // 16 : hi // 16]))
-                if u == 1:
-                    nc.gpsimd.tensor_copy(picked[0][:, lo:hi, :], loose[:, :, lo:hi].rearrange("p u n -> p n u"))
-            nc.vector.tensor_copy(picked[1][:, :, u], pairs[:].indirect(entries(1)))
+        picked = [
+            keep.tile([P, X_VECTOR, PACK], BF16, name="picked_v", align_bytes=64),
+            keep.tile([P, S - X_VECTOR, PACK], BF16, name="picked_s", align_bytes=64),
+        ]
+        for j in range(PACK):
+            nc.vector.tensor_copy(picked[0][:, :, j], planes[j][:].indirect(entries(0, X_VECTOR)))
+            nc.scalar.activation(picked[1][:, :, j], planes[j][:].indirect(entries(X_VECTOR, S)), ACT.Copy)
 
         x_codes, x_plane = {}, {}
 
         def quantize_picked(lo, hi, codes):
             x_codes[lo] = codes
             x_plane[lo] = keep.tile([P, hi - lo], U8, name=f"x_plane{lo}", align_bytes=64)
-            g, first = divmod(lo, HALF)
+            g = 0 if lo < X_VECTOR else 1
+            first = lo - g * X_VECTOR
             nc.vector.quantize_mx(
                 out=codes.bitcast(FP8X4),
                 scales=x_plane[lo][:],
-                in_=picked[g][:, first : first + hi - lo, :].rearrange("p n u -> p (n u)").bitcast(BF16),
+                in_=picked[g][:, first : first + hi - lo, :].rearrange("p n j -> p (n j)"),
             )
 
-        quantize_picked(0, 256, keep.tile([P, 256], U32, name="x_codes0", align_bytes=64)[:])
+        quantize_picked(0, X_VECTOR, keep.tile([P, X_VECTOR], U32, name="x_codes_first", align_bytes=64)[:])
 
         w_codes, w_plane = [], []
         for i in range(2):
+            halves = [
+                placed.tile([P, PACK, P // 2, PACK], BF16, name=f"w_half{i}{h}", offset=12288 + 2048 * (2 * i + h), align_bytes=64)
+                for h in range(2)
+            ]
+            for q, (lo, hi, engine) in enumerate(W_PIECES[i]):
+                half, start = divmod(lo, H // 2)
+                dst = halves[half][:, :, start // PACK : (start + hi - lo) // PACK, :].rearrange("p t m j -> p m t j")
+                src = w_raw[i, q][:].rearrange("p j (m t) -> p m t j", t=PACK)
+                if engine == "vector":
+                    nc.vector.tensor_copy(dst, src)
+                else:
+                    nc.scalar.copy(dst.rearrange("p m t j -> p m j t"), src.rearrange("p m t j -> p m j t"))
             if i == 0:
-                whole = keep.tile([P, PACK, P, PACK], BF16, name="w1_grouped", tag="w_grouped", align_bytes=64)
-                halves = [whole[:, :, : P // 2, :], whole[:, :, P // 2 :, :]]
-            else:
-                halves = [
-                    keep.tile([P, PACK, P // 2, PACK], BF16, name="w3_low", align_bytes=64)[:],
-                    keep.tile([P, PACK, P // 2, PACK], BF16, name="w3_high", tag="w_grouped", align_bytes=64)[:],
-                ]
-            for q, (first, last, shares) in enumerate(W_PIECES[i]):
-                for lo, hi, engine in shares:
-                    if i == 0:
-                        dst = whole[:, :, lo // PACK : hi // PACK, :]
-                    else:
-                        half, start = divmod(lo, H // 2)
-                        dst = halves[half][:, :, start // PACK : (start + hi - lo) // PACK, :]
-                    dst = dst.rearrange("p t m j -> p m t j")
-                    src = w_raw[i, q][:, :, lo - first : hi - first].rearrange("p j (m t) -> p m t j", t=PACK)
-                    if engine == "vector":
-                        nc.vector.tensor_copy(dst, src)
-                    else:
-                        nc.scalar.copy(dst.rearrange("p m t j -> p m j t"), src.rearrange("p m t j -> p m j t"))
+                quantize_picked(X_LAST, S, keep.tile([P, S - X_LAST], U32, name="x_codes_last", tag="w_raw00", align_bytes=64)[:])
             codes = keep.tile([P, H], U32, name=f"w_codes{i}", tag=("w_codes0", "w_raw11")[i], align_bytes=64)
             plane = keep.tile([P, H], U8, name=f"w_plane{i}", align_bytes=64)
-            calls = [
-                (P * t + half * (P // 2), P // 2, halves[half][:, t].rearrange("p m j -> p (m j)"))
-                for half in range(2)
-                for t in range(PACK)
-            ]
-            for lo, width, values in calls:
-                nc.vector.quantize_mx(out=codes[:, lo : lo + width].bitcast(FP8X4), scales=plane[:, lo : lo + width], in_=values)
+            for half in range(2):
+                for t in range(PACK):
+                    cols = slice(P * t + half * (P // 2), P * t + (half + 1) * (P // 2))
+                    nc.vector.quantize_mx(
+                        out=codes[:, cols].bitcast(FP8X4),
+                        scales=plane[:, cols],
+                        in_=halves[half][:, t].rearrange("p m j -> p (m j)"),
+                    )
             w_codes.append(codes)
             w_plane.append(plane)
-            if i == 0:
-                quantize_picked(256, 384, keep.tile([P, CHUNK], U32, name="x_codes2", tag="w_raw02", align_bytes=64)[:])
 
-        later_codes = keep.tile([P, S - 384], U32, name="x_codes_later", tag="w_grouped", align_bytes=64)
-        quantize_picked(384, HALF, later_codes[:, : HALF - 384])
-        quantize_picked(HALF, S, later_codes[:, HALF - 384 :])
+        quantize_picked(X_VECTOR, X_LAST, placed.tile([P, X_LAST - X_VECTOR], U32, name="x_codes_middle", offset=12288 + 2048 * 3 - 512, align_bytes=64)[:])
 
         def up(i, n):
             g = max(lo for lo in x_codes if lo <= n * CHUNK)
-            acc = psum_up.tile([P, PACK, CHUNK], F32, name=f"up{BANKS[i][n]}", tag=f"up{BANKS[i][n]}")
+            bank = BANKS[i][n]
+            acc = psum.tile([P, PACK, CHUNK], F32, name=f"up{bank}", tag=f"up{bank}")
             cols = slice(n * CHUNK - g, (n + 1) * CHUNK - g)
             for t in range(PACK) if n == 0 else (3, 0, 1, 2):
                 nc.tensor.matmul_mx(
@@ -175,85 +153,80 @@ def tile_picked_modres_glusilu_l_kernel(tc, xT, gate, res, w1, w3, w2_words, w2_
                 )
             return acc[:].rearrange("p t n -> p n t")
 
-        hidden = [
-            keep.tile([P, 2 * CHUNK, PACK], BF16, name=f"hidden{r}", tag=f"hidden{r}", align_bytes=64)
-            for r in range(S // (2 * CHUNK))
+        act, hidden, y = {}, {}, {}
+        late = placed.tile([P, 3 * PIECE], F32, name="late", offset=8704, align_bytes=64)
+        early = [
+            keep.tile([P, PIECE], F32, name="early0"),
+            placed.tile([P, PIECE], F32, name="early1", offset=2560, align_bytes=64),
         ]
-        act, y = {}, {}
-        first_acts = keep.tile([P, UP_BANKS, CHUNK, PACK], F32, name="first_acts", tag="w_raw10", align_bytes=64)
         update = keep.tile([P, S], F32, name="update")
 
         def silu(n):
-            if n < UP_BANKS:
-                act[n] = first_acts[:, n, :, :]
+            if n < A_BANKS:
+                act[n] = placed.tile([P, CHUNK, PACK], F32, name=f"act{n}", offset=ACT_PLACES[n], align_bytes=64)[:]
+            elif n == S // CHUNK - 1:
+                act[n] = late[:, LATE_SCALAR + CHUNK : LATE_SCALAR + CHUNK + 2 * PIECE].rearrange("p (n t) -> p n t", t=PACK)
             else:
                 act[n] = keep.tile([P, CHUNK, PACK], F32, name=f"act{n}", tag=f"act{n}", align_bytes=64)[:]
             nc.scalar.activation(act[n], up(0, n), ACT.Silu)
 
         def gated(n):
-            dst = hidden[n // 2][:, n % 2 * CHUNK : (n % 2 + 1) * CHUNK, :]
-            nc.vector.tensor_tensor(dst, up(1, n), act[n], ALU.mult)
+            k = n // 2
+            if k not in hidden:
+                if k == 1:
+                    hidden[k] = placed.tile([P, PIECE, PACK], BF16, name="hidden1", offset=ACT_PLACES[1], align_bytes=64)
+                else:
+                    hidden[k] = keep.tile([P, PIECE, PACK], BF16, name=f"hidden{k}", tag=f"act{2 * k - 1}", align_bytes=64)
+            nc.vector.tensor_tensor(hidden[k][:, n % 2 * CHUNK : (n % 2 + 1) * CHUNK, :], up(1, n), act[n], ALU.mult)
 
-        def down(k, tag):
-            lo, hi, engine = PIECES[k]
-            codes = keep.tile([P, hi - lo], U32, name=f"h_codes{k}", tag=tag, align_bytes=64)
-            plane = keep.tile([P, hi - lo], U8, name=f"h_plane{k}", align_bytes=64)
-            for first in range(0, hi - lo, 2 * CHUNK):
-                cols = slice(first, first + 2 * CHUNK)
-                y[lo + first] = psum_down.tile([P, 2 * CHUNK], F32, name="y")
-                nc.vector.quantize_mx(
-                    out=codes[:, cols].bitcast(FP8X4),
-                    scales=plane[:, cols],
-                    in_=hidden[(lo + first) // (2 * CHUNK)][:].rearrange("p n t -> p (n t)"),
-                )
-                nc.tensor.matmul_mx(
-                    out=y[lo + first][:],
-                    lhsT=w2_codes[:].bitcast(FP4X4),
-                    lhsT_scale=w2_plane[:],
-                    rhs=codes[:, cols].bitcast(FP8X4),
-                    rhs_scale=plane[:, cols],
-                    start=True,
-                    stop=True,
-                )
+        def down(k):
+            codes = keep.tile([P, PIECE], U32, name=f"h_codes{k}", align_bytes=64)
+            plane = keep.tile([P, PIECE], U8, name=f"h_plane{k}", align_bytes=64)
+            nc.vector.quantize_mx(out=codes[:].bitcast(FP8X4), scales=plane[:], in_=hidden[k][:].rearrange("p n t -> p (n t)"))
+            y[k] = psum.tile([P, PIECE], F32, name="y", tag="y")
+            nc.tensor.matmul_mx(
+                out=y[k][:],
+                lhsT=w2_codes[:].bitcast(FP4X4),
+                lhsT_scale=w2_plane[:],
+                rhs=codes[:].bitcast(FP8X4),
+                rhs_scale=plane[:],
+                start=True,
+                stop=True,
+            )
 
         def weigh(k):
-            lo, hi, engine = PIECES[k]
-            for first in range(lo, hi, 2 * CHUNK):
-                cols = slice(first, first + 2 * CHUNK)
-                nc.vector.tensor_tensor(update[:, cols], y[first][:], gates[:, cols], ALU.mult)
+            g, first = divmod(k * PIECE, S // 2)
+            nc.vector.tensor_tensor(update[:, k * PIECE : (k + 1) * PIECE], y[k][:], gates[g][:, first : first + PIECE], ALU.mult)
 
-        def put(k, old, adder):
-            lo, hi, engine = PIECES[k]
-            places = window[:].indirect(offsets[:, lo // 16 : hi // 16])
-            if engine == "vector":
-                nc.vector.tensor_tensor(places, old[:, lo:hi], update[:, lo:hi], ALU.add)
-            else:
-                total = keep.tile([P, hi - lo], F32, name=f"total{k}")
-                adder.tensor_tensor(total[:], old[:, lo:hi], update[:, lo:hi], ALU.add)
-                nc.scalar.activation(places, total[:], ACT.Copy)
+        def put(k):
+            cols = slice(k * PIECE, (k + 1) * PIECE)
+            total = keep.tile([P, PIECE], F32, name=f"total{k}")
+            nc.gpsimd.tensor_tensor(total[:], early[k][:], update[:, cols], ALU.add)
+            nc.scalar.activation(window[:].indirect(entries(k * PIECE, (k + 1) * PIECE)), total[:], ACT.Copy)
 
-        for n in range(UP_BANKS):
+        half = S // 2
+        split = LATE_SCALAR + CHUNK
+        for n in range(A_BANKS):
             silu(n)
-        for n in range(UP_BANKS):
-            gated(n)
-            silu(UP_BANKS + n)
-        old = keep.tile([P, S], F32, name="old", tag="w_raw02", align_bytes=64)
-        nc.scalar.activation(old[:, :SCALAR_GATHER], source[:].indirect(offsets[:, : SCALAR_GATHER // 16]), ACT.Copy)
-        down(0, "h_codes0")
-        gated(3)
-        silu(6)
-        silu(7)
-        gated(4)
-        weigh(0)
-        down(1, "h_codes1")
-        put(0, old, nc.vector)
-        gated(5)
-        weigh(1)
-        put(1, old, nc.gpsimd)
-        gated(6)
-        gated(7)
-        down(2, "act6")
-        nc.vector.tensor_copy(old[:, SCALAR_GATHER:], source[:].indirect(offsets[:, SCALAR_GATHER // 16 :]))
-        weigh(2)
-        put(2, old, nc.vector)
+        nc.scalar.activation(early[0][:], source[:].indirect(entries(0, PIECE)), ACT.Copy)
+        gated(0)
+        gated(1)
+        for n in range(A_BANKS, 2 * A_BANKS):
+            silu(n)
+        nc.vector.tensor_copy(late[:, LATE_SCALAR:split], source[:].indirect(entries(half + LATE_SCALAR, half + split)))
+        for k in range(S // PIECE):
+            down(k)
+            if k < S // PIECE - 1:
+                gated(2 * k + 2)
+                gated(2 * k + 3)
+                if k == 0:
+                    nc.scalar.activation(early[1][:], source[:].indirect(entries(PIECE, half)), ACT.Copy)
+                    silu(6)
+                    silu(7)
+            else:
+                nc.vector.tensor_copy(late[:, split:half], source[:].indirect(entries(half + split, S)))
+            weigh(k)
+            if k < 2:
+                put(k)
+        nc.vector.tensor_tensor(window[:].indirect(entries(half, S)), late[:, :half], update[:, half:], ALU.add)
         nc.sync.dma_start(out, window[:])

@@ -21,11 +21,16 @@ PACK = 4
 CHUNK = 128
 PIECE = 256
 X_VECTOR = 384
-X_LAST = 640
+X_LAST = 768
 LATE_SCALAR = 0
 W_PIECES = (
-    ((0, 256, "vector"), (256, 512, "scalar")),
-    ((0, 256, "scalar"), (256, 384, "vector"), (384, 512, "vector")),
+    ((0, 256, ((0, 256, "vector"),)), (256, 384, ((256, 384, "vector"),)), (384, 512, ((384, 512, "scalar"),))),
+    (
+        (0, 128, ((0, 128, "scalar"),)),
+        (128, 256, ((128, 256, "scalar"),)),
+        (256, 384, ((256, 384, "vector"),)),
+        (384, 512, ((384, 512, "vector"),)),
+    ),
 )
 A_BANKS, B_BANKS = 3, 4
 BANKS = ((0, 1, 2, 0, 1, 2, 4, 6), (3, 4, 5, 6, 3, 0, 5, 3))
@@ -68,19 +73,18 @@ def tile_picked_modres_glusilu_l_kernel(tc, xT, gate, res, w1, w3, w2_words, w2_
         w_raw = {}
         for i, w in enumerate((w1, w3)):
             w_rows = w.rearrange("(p j) c -> p j c", j=PACK)
-            for q, (lo, hi, engine) in enumerate(W_PIECES[i]):
-                if (i, q) == (1, 0):
-                    w_raw[i, q] = placed.tile([P, PACK, hi - lo], F32, name="w_raw10", offset=4096, align_bytes=64)
+            for q, (lo, hi, shares) in enumerate(W_PIECES[i]):
+                if (i, q) == (1, 1):
+                    w_raw[i, q] = placed.tile([P, PACK, hi - lo], F32, name="w_raw11", offset=6144, align_bytes=64)
                 else:
                     w_raw[i, q] = keep.tile([P, PACK, hi - lo], F32, name=f"w_raw{i}{q}", tag=f"w_raw{i}{q}", align_bytes=64)
                 nc.sync.dma_start(w_raw[i, q][:], w_rows[:, :, lo:hi])
         source = keep.tile([P, T], F32, name="source")
         nc.sync.dma_start(source[:], res)
-        gates = [keep.tile([P, S // 2], F32, name=f"gates{g}") for g in range(2)]
-        nc.sync.dma_start(gates[0][:], gate[:, : S // 2])
+        gates = keep.tile([P, S], F32, name="gates")
+        nc.sync.dma_start(gates[:], gate)
         window = keep.tile([P, T], F32, name="window")
         nc.sync.dma_start(window[:], res)
-        nc.sync.dma_start(gates[1][:], gate[:, S // 2 :])
 
         picked = [
             keep.tile([P, X_VECTOR, PACK], BF16, name="picked_v", align_bytes=64),
@@ -111,30 +115,37 @@ def tile_picked_modres_glusilu_l_kernel(tc, xT, gate, res, w1, w3, w2_words, w2_
                 placed.tile([P, PACK, P // 2, PACK], BF16, name=f"w_half{i}{h}", offset=12288 + 2048 * (2 * i + h), align_bytes=64)
                 for h in range(2)
             ]
-            for q, (lo, hi, engine) in enumerate(W_PIECES[i]):
-                half, start = divmod(lo, H // 2)
-                dst = halves[half][:, :, start // PACK : (start + hi - lo) // PACK, :].rearrange("p t m j -> p m t j")
-                src = w_raw[i, q][:].rearrange("p j (m t) -> p m t j", t=PACK)
-                if engine == "vector":
-                    nc.vector.tensor_copy(dst, src)
-                else:
-                    nc.scalar.copy(dst.rearrange("p m t j -> p m j t"), src.rearrange("p m t j -> p m j t"))
-            if i == 0:
-                quantize_picked(X_LAST, S, keep.tile([P, S - X_LAST], U32, name="x_codes_last", tag="w_raw00", align_bytes=64)[:])
-            codes = keep.tile([P, H], U32, name=f"w_codes{i}", tag=("w_codes0", "w_raw11")[i], align_bytes=64)
+            for q, (first, last, shares) in enumerate(W_PIECES[i]):
+                for lo, hi, engine in shares:
+                    half, start = divmod(lo, H // 2)
+                    dst = halves[half][:, :, start // PACK : (start + hi - lo) // PACK, :].rearrange("p t m j -> p m t j")
+                    src = w_raw[i, q][:, :, lo - first : hi - first].rearrange("p j (m t) -> p m t j", t=PACK)
+                    if engine == "vector":
+                        nc.vector.tensor_copy(dst, src)
+                    else:
+                        nc.scalar.copy(dst.rearrange("p m t j -> p m j t"), src.rearrange("p m t j -> p m j t"))
+            pairs = [
+                keep.tile([P, H // 2], U32, name=f"w_codes{i}{u}", tag="w_raw12" if (i, u) == (1, 1) else f"w_codes{i}{u}", align_bytes=64)
+                for u in range(2)
+            ]
+            codes = [pairs[t // 2][:, t % 2 * P : (t % 2 + 1) * P] for t in range(PACK)]
             plane = keep.tile([P, H], U8, name=f"w_plane{i}", align_bytes=64)
             for half in range(2):
                 for t in range(PACK):
                     cols = slice(P * t + half * (P // 2), P * t + (half + 1) * (P // 2))
                     nc.vector.quantize_mx(
-                        out=codes[:, cols].bitcast(FP8X4),
+                        out=codes[t][:, half * (P // 2) : (half + 1) * (P // 2)].bitcast(FP8X4),
                         scales=plane[:, cols],
                         in_=halves[half][:, t].rearrange("p m j -> p (m j)"),
                     )
             w_codes.append(codes)
             w_plane.append(plane)
+            if i == 0:
+                later = keep.tile([P, S - X_LAST + CHUNK], U32, name="x_codes_later", tag="w_raw02", align_bytes=64)
+                quantize_picked(X_VECTOR, X_VECTOR + CHUNK, later[:, :CHUNK])
+                quantize_picked(X_LAST, S, later[:, CHUNK:])
 
-        quantize_picked(X_VECTOR, X_LAST, placed.tile([P, X_LAST - X_VECTOR], U32, name="x_codes_middle", offset=12288 + 2048 * 3 - 512, align_bytes=64)[:])
+        quantize_picked(X_LAST - PIECE, X_LAST, placed.tile([P, PIECE], U32, name="x_codes_middle", offset=12288 + 2048 * 3 - 512, align_bytes=64)[:])
 
         def up(i, n):
             g = max(lo for lo in x_codes if lo <= n * CHUNK)
@@ -144,7 +155,7 @@ def tile_picked_modres_glusilu_l_kernel(tc, xT, gate, res, w1, w3, w2_words, w2_
             for t in range(PACK) if n == 0 else (3, 0, 1, 2):
                 nc.tensor.matmul_mx(
                     out=acc[:, t, :],
-                    lhsT=w_codes[i][:, t * P : (t + 1) * P].bitcast(FP8X4),
+                    lhsT=w_codes[i][t].bitcast(FP8X4),
                     lhsT_scale=w_plane[i][:, t * P : (t + 1) * P],
                     rhs=x_codes[g][:, cols].bitcast(FP8X4),
                     rhs_scale=x_plane[g][:, cols],
@@ -154,11 +165,8 @@ def tile_picked_modres_glusilu_l_kernel(tc, xT, gate, res, w1, w3, w2_words, w2_
             return acc[:].rearrange("p t n -> p n t")
 
         act, hidden, y = {}, {}, {}
-        late = placed.tile([P, 3 * PIECE], F32, name="late", offset=8704, align_bytes=64)
-        early = [
-            keep.tile([P, PIECE], F32, name="early0"),
-            placed.tile([P, PIECE], F32, name="early1", offset=2560, align_bytes=64),
-        ]
+        late = keep.tile([P, 3 * PIECE], F32, name="late", align_bytes=64)
+        early = keep.tile([P, 2 * PIECE], F32, name="early")
         update = keep.tile([P, S], F32, name="update")
 
         def silu(n):
@@ -182,7 +190,12 @@ def tile_picked_modres_glusilu_l_kernel(tc, xT, gate, res, w1, w3, w2_words, w2_
         def down(k):
             codes = keep.tile([P, PIECE], U32, name=f"h_codes{k}", align_bytes=64)
             plane = keep.tile([P, PIECE], U8, name=f"h_plane{k}", align_bytes=64)
-            nc.vector.quantize_mx(out=codes[:].bitcast(FP8X4), scales=plane[:], in_=hidden[k][:].rearrange("p n t -> p (n t)"))
+            for lo, hi in ((0, CHUNK), (CHUNK, PIECE)) if k == 0 else ((0, PIECE),):
+                nc.vector.quantize_mx(
+                    out=codes[:, lo:hi].bitcast(FP8X4),
+                    scales=plane[:, lo:hi],
+                    in_=hidden[k][:, lo:hi, :].rearrange("p n t -> p (n t)"),
+                )
             y[k] = psum.tile([P, PIECE], F32, name="y", tag="y")
             nc.tensor.matmul_mx(
                 out=y[k][:],
@@ -195,32 +208,31 @@ def tile_picked_modres_glusilu_l_kernel(tc, xT, gate, res, w1, w3, w2_words, w2_
             )
 
         def weigh(k):
-            g, first = divmod(k * PIECE, S // 2)
-            nc.vector.tensor_tensor(update[:, k * PIECE : (k + 1) * PIECE], y[k][:], gates[g][:, first : first + PIECE], ALU.mult)
+            cols = slice(k * PIECE, (k + 1) * PIECE)
+            nc.vector.tensor_tensor(update[:, cols], y[k][:], gates[:, cols], ALU.mult)
 
         def put(k):
             cols = slice(k * PIECE, (k + 1) * PIECE)
             total = keep.tile([P, PIECE], F32, name=f"total{k}")
-            nc.gpsimd.tensor_tensor(total[:], early[k][:], update[:, cols], ALU.add)
+            nc.gpsimd.tensor_tensor(total[:], early[:, cols], update[:, cols], ALU.add)
             nc.scalar.activation(window[:].indirect(entries(k * PIECE, (k + 1) * PIECE)), total[:], ACT.Copy)
 
         half = S // 2
         split = LATE_SCALAR + CHUNK
-        for n in range(A_BANKS):
+        for n in range(A_BANKS + 1):
             silu(n)
-        nc.scalar.activation(early[0][:], source[:].indirect(entries(0, PIECE)), ACT.Copy)
+        nc.scalar.activation(early[:], source[:].indirect(entries(0, half)), ACT.Copy)
+        nc.scalar.activation(late[:, :split], source[:].indirect(entries(half, half + split)), ACT.Copy)
         gated(0)
         gated(1)
-        for n in range(A_BANKS, 2 * A_BANKS):
+        for n in range(A_BANKS + 1, 2 * A_BANKS):
             silu(n)
-        nc.vector.tensor_copy(late[:, LATE_SCALAR:split], source[:].indirect(entries(half + LATE_SCALAR, half + split)))
         for k in range(S // PIECE):
             down(k)
             if k < S // PIECE - 1:
                 gated(2 * k + 2)
                 gated(2 * k + 3)
                 if k == 0:
-                    nc.scalar.activation(early[1][:], source[:].indirect(entries(PIECE, half)), ACT.Copy)
                     silu(6)
                     silu(7)
             else:

@@ -33,7 +33,7 @@ W_PIECES = (
     ),
 )
 A_BANKS, B_BANKS = 3, 4
-BANKS = ((0, 1, 2, 0, 1, 2, 4, 6), (3, 4, 5, 6, 3, 0, 5, 3))
+BANKS = ((0, 1, 2, 0, 3, 4, 5, 6), (3, 4, 5, 6, 1, 2, 0, 1))
 ACT_PLACES = (7168, 4608, 2560)
 
 

from contextlib import ExitStack

import concourse.mybir as mybir

K, T, S, H, N = 512, 2048, 1024, 512, 128
FLOPS = 2 * S * (2 * K * H + H * N)

F32 = mybir.dt.float32
BF16 = mybir.dt.bfloat16
I32 = mybir.dt.int32
U32 = mybir.dt.uint32
U16 = mybir.dt.uint16
U8 = mybir.dt.uint8
FP8X4 = mybir.dt.float8_e4m3fn_x4
FP4X4 = mybir.dt.float4_e2m1fn_x4
ALU = mybir.AluOpType
ACT = mybir.ActivationFunctionType

P = 128
PACK = 4
CHUNK = 128
PIECE = 256
X_VECTOR = 384
X_LAST = 768
LATE_SCALAR = 0
W_PIECES = (
    ((0, 256, ((0, 256, "vector"),)), (256, 384, ((256, 384, "vector"),)), (384, 512, ((384, 512, "scalar"),))),
    (
        (0, 128, ((0, 128, "scalar"),)),
        (128, 256, ((128, 256, "scalar"),)),
        (256, 384, ((256, 384, "vector"),)),
        (384, 512, ((384, 512, "vector"),)),
    ),
)
A_BANKS, B_BANKS = 3, 4
BANKS = ((0, 1, 2, 0, 3, 4, 5, 6), (3, 4, 5, 6, 1, 2, 0, 1))
ACT_PLACES = (7168, 4608, 2560)


def tile_picked_modres_glusilu_l_kernel(tc, xT, gate, res, w1, w3, w2_words, w2_scales, offs, out):
    nc = tc.nc
    with ExitStack() as ctx:
        keep = ctx.enter_context(tc.tile_pool(name="keep", bufs=1))
        placed = ctx.enter_context(tc.tile_pool(name="placed", bufs=1))
        psum = ctx.enter_context(tc.psum_pool(name="psum", bufs=1))

        offsets = keep.tile([P, S // 16], U16, name="offsets")
        x_rows = xT.rearrange("(p j) n -> p j n", j=PACK)
        w2_codes = keep.tile([P, 2 * N], U8, name="w2_codes", align_bytes=64)
        w2_plane = keep.tile([P, N], U8, name="w2_plane", align_bytes=64)

        def entries(lo, hi):
            return offsets[:, lo // 16 : hi // 16]

        warm = keep.tile([P, 2], F32, name="warm")
        nc.gpsimd.memset(warm[:, 0:1], 0.0)
        nc.scalar.activation(warm[:, 1:2], warm[:, 0:1], ACT.Silu)

        nc.gpsimd.memset(w2_plane[:].bitcast(I32), 0)
        nc.gpsimd.dma_start(w2_codes[:].bitcast(I32), w2_words[0].bitcast(I32))
        for quadrant in range(4):
            nc.gpsimd.dma_start(
                w2_plane[32 * quadrant : 32 * quadrant + 4, :].bitcast(I32),
                w2_scales[0, 4 * quadrant : 4 * quadrant + 4, :].bitcast(I32),
            )

        planes = []
        for j in range(PACK):
            planes.append(keep.tile([P, T], F32, name=f"x_raw{j}"))
            nc.sync.dma_start(planes[j][:], x_rows[:, j, :])
            if j == 0:
                nc.sync.dma_start(offsets[:], offs)
        w_raw = {}
        for i, w in enumerate((w1, w3)):
            w_rows = w.rearrange("(p j) c -> p j c", j=PACK)
            for q, (lo, hi, shares) in enumerate(W_PIECES[i]):
                if (i, q) == (1, 1):
                    w_raw[i, q] = placed.tile([P, PACK, hi - lo], F32, name="w_raw11", offset=6144, align_bytes=64)
                else:
                    w_raw[i, q] = keep.tile([P, PACK, hi - lo], F32, name=f"w_raw{i}{q}", tag=f"w_raw{i}{q}", align_bytes=64)
                nc.sync.dma_start(w_raw[i, q][:], w_rows[:, :, lo:hi])
        source = keep.tile([P, T], F32, name="source")
        nc.sync.dma_start(source[:], res)
        gates = keep.tile([P, S], F32, name="gates")
        nc.sync.dma_start(gates[:], gate)
        window = keep.tile([P, T], F32, name="window")
        nc.sync.dma_start(window[:], res)

        picked = [
            keep.tile([P, X_VECTOR, PACK], BF16, name="picked_v", align_bytes=64),
            keep.tile([P, S - X_VECTOR, PACK], BF16, name="picked_s", align_bytes=64),
        ]
        for j in range(PACK):
            nc.vector.tensor_copy(picked[0][:, :, j], planes[j][:].indirect(entries(0, X_VECTOR)))
            nc.scalar.activation(picked[1][:, :, j], planes[j][:].indirect(entries(X_VECTOR, S)), ACT.Copy)

        x_codes, x_plane = {}, {}

        def quantize_picked(lo, hi, codes):
            x_codes[lo] = codes
            x_plane[lo] = keep.tile([P, hi - lo], U8, name=f"x_plane{lo}", align_bytes=64)
            g = 0 if lo < X_VECTOR else 1
            first = lo - g * X_VECTOR
            nc.vector.quantize_mx(
                out=codes.bitcast(FP8X4),
                scales=x_plane[lo][:],
                in_=picked[g][:, first : first + hi - lo, :].rearrange("p n j -> p (n j)"),
            )

        quantize_picked(0, X_VECTOR, keep.tile([P, X_VECTOR], U32, name="x_codes_first", align_bytes=64)[:])

        w_codes, w_plane = [], []
        for i in range(2):
            halves = [
                placed.tile([P, PACK, P // 2, PACK], BF16, name=f"w_half{i}{h}", offset=12288 + 2048 * (2 * i + h), align_bytes=64)
                for h in range(2)
            ]
            for q, (first, last, shares) in enumerate(W_PIECES[i]):
                for lo, hi, engine in shares:
                    half, start = divmod(lo, H // 2)
                    dst = halves[half][:, :, start // PACK : (start + hi - lo) // PACK, :].rearrange("p t m j -> p m t j")
                    src = w_raw[i, q][:, :, lo - first : hi - first].rearrange("p j (m t) -> p m t j", t=PACK)
                    if engine == "vector":
                        nc.vector.tensor_copy(dst, src)
                    else:
                        nc.scalar.copy(dst.rearrange("p m t j -> p m j t"), src.rearrange("p m t j -> p m j t"))
            pairs = [
                keep.tile([P, H // 2], U32, name=f"w_codes{i}{u}", tag="w_raw12" if (i, u) == (1, 1) else f"w_codes{i}{u}", align_bytes=64)
                for u in range(2)
            ]
            codes = [pairs[t // 2][:, t % 2 * P : (t % 2 + 1) * P] for t in range(PACK)]
            plane = keep.tile([P, H], U8, name=f"w_plane{i}", align_bytes=64)
            for half in range(2):
                for t in range(PACK):
                    cols = slice(P * t + half * (P // 2), P * t + (half + 1) * (P // 2))
                    nc.vector.quantize_mx(
                        out=codes[t][:, half * (P // 2) : (half + 1) * (P // 2)].bitcast(FP8X4),
                        scales=plane[:, cols],
                        in_=halves[half][:, t].rearrange("p m j -> p (m j)"),
                    )
            w_codes.append(codes)
            w_plane.append(plane)
            if i == 0:
                later = keep.tile([P, S - X_LAST + CHUNK], U32, name="x_codes_later", tag="w_raw02", align_bytes=64)
                quantize_picked(X_VECTOR, X_VECTOR + CHUNK, later[:, :CHUNK])
                quantize_picked(X_LAST, S, later[:, CHUNK:])

        quantize_picked(X_LAST - PIECE, X_LAST, placed.tile([P, PIECE], U32, name="x_codes_middle", offset=12288 + 2048 * 3 - 512, align_bytes=64)[:])

        def up(i, n):
            g = max(lo for lo in x_codes if lo <= n * CHUNK)
            bank = BANKS[i][n]
            acc = psum.tile([P, PACK, CHUNK], F32, name=f"up{bank}", tag=f"up{bank}")
            cols = slice(n * CHUNK - g, (n + 1) * CHUNK - g)
            for t in range(PACK) if n == 0 else (3, 0, 1, 2):
                nc.tensor.matmul_mx(
                    out=acc[:, t, :],
                    lhsT=w_codes[i][t].bitcast(FP8X4),
                    lhsT_scale=w_plane[i][:, t * P : (t + 1) * P],
                    rhs=x_codes[g][:, cols].bitcast(FP8X4),
                    rhs_scale=x_plane[g][:, cols],
                    start=True,
                    stop=True,
                )
            return acc[:].rearrange("p t n -> p n t")

        act, hidden, y = {}, {}, {}
        late = keep.tile([P, 3 * PIECE], F32, name="late", align_bytes=64)
        early = keep.tile([P, 2 * PIECE], F32, name="early")
        update = keep.tile([P, S], F32, name="update")

        def silu(n):
            if n < A_BANKS:
                act[n] = placed.tile([P, CHUNK, PACK], F32, name=f"act{n}", offset=ACT_PLACES[n], align_bytes=64)[:]
            elif n == S // CHUNK - 1:
                act[n] = late[:, LATE_SCALAR + CHUNK : LATE_SCALAR + CHUNK + 2 * PIECE].rearrange("p (n t) -> p n t", t=PACK)
            else:
                act[n] = keep.tile([P, CHUNK, PACK], F32, name=f"act{n}", tag=f"act{n}", align_bytes=64)[:]
            nc.scalar.activation(act[n], up(0, n), ACT.Silu)

        def gated(n):
            k = n // 2
            if k not in hidden:
                if k == 1:
                    hidden[k] = placed.tile([P, PIECE, PACK], BF16, name="hidden1", offset=ACT_PLACES[1], align_bytes=64)
                else:
                    hidden[k] = keep.tile([P, PIECE, PACK], BF16, name=f"hidden{k}", tag=f"act{2 * k - 1}", align_bytes=64)
            nc.vector.tensor_tensor(hidden[k][:, n % 2 * CHUNK : (n % 2 + 1) * CHUNK, :], up(1, n), act[n], ALU.mult)

        def down(k):
            codes = keep.tile([P, PIECE], U32, name=f"h_codes{k}", align_bytes=64)
            plane = keep.tile([P, PIECE], U8, name=f"h_plane{k}", align_bytes=64)
            for lo, hi in ((0, CHUNK), (CHUNK, PIECE)) if k == 0 else ((0, PIECE),):
                nc.vector.quantize_mx(
                    out=codes[:, lo:hi].bitcast(FP8X4),
                    scales=plane[:, lo:hi],
                    in_=hidden[k][:, lo:hi, :].rearrange("p n t -> p (n t)"),
                )
            y[k] = psum.tile([P, PIECE], F32, name="y", tag="y")
            nc.tensor.matmul_mx(
                out=y[k][:],
                lhsT=w2_codes[:].bitcast(FP4X4),
                lhsT_scale=w2_plane[:],
                rhs=codes[:].bitcast(FP8X4),
                rhs_scale=plane[:],
                start=True,
                stop=True,
            )

        def weigh(k):
            cols = slice(k * PIECE, (k + 1) * PIECE)
            nc.vector.tensor_tensor(update[:, cols], y[k][:], gates[:, cols], ALU.mult)

        def put(k):
            cols = slice(k * PIECE, (k + 1) * PIECE)
            total = keep.tile([P, PIECE], F32, name=f"total{k}")
            nc.gpsimd.tensor_tensor(total[:], early[:, cols], update[:, cols], ALU.add)
            nc.scalar.activation(window[:].indirect(entries(k * PIECE, (k + 1) * PIECE)), total[:], ACT.Copy)

        half = S // 2
        split = LATE_SCALAR + CHUNK
        for n in range(A_BANKS + 1):
            silu(n)
        nc.scalar.activation(early[:], source[:].indirect(entries(0, half)), ACT.Copy)
        nc.scalar.activation(late[:, :split], source[:].indirect(entries(half, half + split)), ACT.Copy)
        gated(0)
        gated(1)
        for n in range(A_BANKS + 1, 2 * A_BANKS):
            silu(n)
        for k in range(S // PIECE):
            down(k)
            if k < S // PIECE - 1:
                gated(2 * k + 2)
                gated(2 * k + 3)
                if k == 0:
                    silu(6)
                    silu(7)
            else:
                nc.vector.tensor_copy(late[:, split:half], source[:].indirect(entries(half + split, S)))
            weigh(k)
            if k < 2:
                put(k)
        nc.vector.tensor_tensor(window[:].indirect(entries(half, S)), late[:, :half], update[:, half:], ALU.add)
        nc.sync.dma_start(out, window[:])
